import numpy as np, ml_dtypes
CORES = [16,17,18,19,32,33,34,35]
N = 8
BF = ml_dtypes.bfloat16
def gentries(a):
    return np.ascontiguousarray(a.reshape(8, 16, -1).transpose(0, 2, 1)).reshape(8, -1)
def gtable(e):
    e = np.asarray(e); return np.ascontiguousarray(e.reshape(8, -1, 16).transpose(0, 2, 1)).reshape(128, -1).astype(np.int32)
M, L, T, H, A, R = 2048, 192, 4, 2048, 10, 1024
W = M + L * T; NONE = 4095
def hashes(w, a):
    u = np.matmul(w.transpose(0, 2, 1), a) & 4095
    return (((u[:, 0] * u[:, 1]) >> 5) + u[:, 1]) & (H - 1)
def some(rng, n, tops):
    return (rng.random((N, 8, 16, n)) * rng.choice(np.array(tops), (N, 8, 1, n))).astype(np.int64)
def places(rng, sizes):
    v = np.zeros((N, 8, L), np.int64)
    for r in range(N):
        for g in range(8):
            pool = rng.permutation(M)[:int(sizes[r, g])]; v[r, g] = pool[rng.integers(0, len(pool), L)]
    return v
def flat(a):
    return np.ascontiguousarray(a.reshape(N, 128, -1)).astype(np.float32).astype(BF)
def pack(X, B, E, x, v, w):
    return {"nodes": flat(X), "book": flat(B), "kids": np.ascontiguousarray(E.reshape(N, 128, M)).astype(np.int32), "cand": flat(x),
            "spot": np.stack([gtable(a) for a in v]), "wts": flat(w)}
def setup_inputs(rng):
    X = some(rng, M, (48, 96, 160, 256)); B = some(rng, H, (96, 160, 256)); x = some(rng, L, (96, 192, 256))
    k = np.minimum(rng.integers(0, 17, (N, 8, 16, M)), rng.integers(0, 17, (N, 8, 16, M)))
    fill = rng.choice(np.array([0.3, 0.6, 0.9, 1.0]), (N, 8, 1, M))
    E = 4096 * k + np.where(rng.random((N, 8, 16, M)) < fill, rng.integers(0, M, (N, 8, 16, M)), NONE)
    v = places(rng, rng.choice(np.array([8, 32, 128, M]), (N, 8)))
    return pack(X, B, E, x, v, rng.integers(0, 16, (N, 8, 16, 2)))
def setup_inputs_spread(rng):
    X = (np.exp2(8 * rng.random((N, 8, 1, M))) * rng.random((N, 8, 16, M))).astype(np.int64)
    x = (np.exp2(8 * rng.random((N, 8, 1, L))) * rng.random((N, 8, 16, L))).astype(np.int64); B = rng.integers(0, 256, (N, 8, 16, H))
    E = 4096 * rng.integers(0, 17, (N, 8, 16, M)) + np.where(rng.random((N, 8, 16, M)) < rng.random((N, 8, 1, M)), rng.integers(0, M, (N, 8, 16, M)), NONE)
    v = np.minimum((M * rng.random((N, 8, L)) ** 3).astype(np.int64), M - 1); w = np.minimum((16 * rng.random((N, 8, 16, 2)) ** 2).astype(np.int64), 15)
    return pack(X, B, E, x, v, w)
def setup_inputs_ends(rng):
    X = 255 * rng.integers(0, 2, (N, 8, 16, M)); B = 255 * rng.integers(0, 2, (N, 8, 16, H)); x = 255 * rng.integers(0, 2, (N, 8, 16, L))
    a = rng.random((N, 8, 1, L)); x = np.where(a < 0.15, 0, np.where(a < 0.4, 255, x))
    X[..., 0] = 0; X[..., M - 1] = 255
    w = 15 * rng.integers(0, 2, (N, 8, 16, 2)); w[:, ::2, 13] = 15; w[:, ::2, 14] = 1; w[:, ::2, 15] = 15; w[:, 7] = 15
    E = 69631 * rng.integers(0, 2, (N, 8, 16, M)); o = rng.random(E.shape)
    E = np.where(o < 0.35, rng.choice(np.array([65536, M - 1, M - 1 + 65536]), E.shape), E)
    E = np.where(o < 0.1, rng.integers(1, M - 16, E.shape) + 65536 * rng.integers(0, 2, E.shape), E)
    E[..., M - 1] = 69631 * rng.integers(0, 2, (N, 8, 16)); E[:, :, 15, M - 1] = M - 1 + 65536; low = rng.integers(0, 8, (N, 8))
    E[:, :, :15, M - 2] = 0; E[:, :, 15, M - 2] = 69631
    for j in range(1, T): E[:, :, :, M - 2 - j] = 65536 + M - 1 - j
    E[:, :, :15, M - 2 - T] = 69631; E[:, :, 15, M - 2 - T] = 0
    v = np.where(rng.random((N, 8, L)) < 0.68, (M - 1) * rng.integers(0, 2, (N, 8, L)), rng.integers(1, M - 16, (N, 8, L)))
    v[:, :, L - 1] = M - 1 - T; x[..., L - 1] = 255
    v[:, :, L - 17] = M - 1; x[..., L - 17] = 255
    v[:, :, L - 33] = M - 2 - T; x[..., L - 33] = 255
    v[:, :, L - 2] = M - 1; x[:, ::2, :, L - 2] = 0; x[:, ::2, 14:, L - 2] = 255; x[:, ::2, 13, L - 2] = 1
    s = rng.integers(0, 2, (N, 8)); s[:, 7] = 1; s[:, 1] = 0
    for r in range(N):
        h = hashes(w[r], np.full((8, 16, 1), 255))[:, 0]
        for g in range(8):
            B[r, g, :, h[g]] = 255 * s[r, g]; E[r, g, low[r, g], M - 1] = 65536
    return pack(X, B, E, x, v, w)
def setup_inputs_corners(rng):
    X = some(rng, M, (2, 64, 256)); B = some(rng, H, (2, 128, 256))
    kind = rng.integers(0, 9, (N, 8, 1, M)); kind[..., 5:6 + T] = 4
    own = np.arange(M); one = rng.integers(0, 16, (N, 8, 1, M)); line = np.arange(16)[:, None]
    c = rng.integers(0, M, (N, 8, 16, M))
    c = np.where(kind == 3, own, np.where(kind == 4, (own + 1) % M, np.where(kind == 5, 0, np.where(kind == 6, M - 1, c))))
    hide = (kind == 0) | ((kind == 2) & (line != one)) | ((kind == 7) & (line == one)) | ((kind == 8) & (rng.random(c.shape) < 0.5))
    m = rng.integers(0, 4, (N, 8, 1, M)); m = np.where(kind == 4, 1, m)
    k = np.where(m == 0, 0, np.where(m == 1, 16, np.where(m == 2, 15, rng.integers(0, 17, c.shape))))
    E = 4096 * k + np.where(hide, NONE, c)
    v = rng.integers(0, M, (N, 8, L)); w = rng.integers(0, 16, (N, 8, 16, 2))
    for r in range(N):
        o = rng.permutation(8); q = rng.permutation(M)
        v[r, o[0]] = 0; v[r, o[1]] = M - 1; v[r, o[2]] = q[:L]; v[r, o[3]] = rng.permutation(np.repeat(q[:L // 2], 2))
        v[r, o[4]] = rng.choice(np.array([5, 0, M - 1, 6]), L); v[r, o[5], ::2] = 5; v[r, o[5], L - 1] = 5
        b = rng.permutation(8)
        w[r, b[0]] = 0; w[r, b[1]] = 15; w[r, b[2], 1:] = 0; w[r, b[2], 0] = 15; w[r, b[3], :15] = 0; w[r, b[3], 15] = 15; w[r, b[4], :, 0] = 0; w[r, b[5], :, 1] = 0
    d = rng.integers(0, 4, (N, 8, 1, L)); x = some(rng, L, (64, 256))
    x = np.where(d == 0, 0, np.where(d == 1, 255, np.where(d == 2, np.take_along_axis(X, v[:, :, None, :], 3), x)))
    return pack(X, B, E, x, v, w)
def full(rng, X, B, E, x, v, r, late):
    n = T - 1 if late else 0; half = rng.permutation(8)
    for g in range(8):
        u = rng.permutation(M)[:L * T].reshape(T, L); e = E[r, g]; v[r, g] = u[0]
        for j in range(n): e[:, u[j]] = 65536 + u[j + 1][None, :]
        if half[g] < 4:
            e[:, u[n]] = NONE + 4096 * rng.integers(0, 17, (16, L))
        else:
            X[r, g] = rng.integers(0, 8, (16, M)); x[r, g] = rng.integers(8, 24, (16, L)); B[r, g] = rng.integers(24, 256, (16, H))
            e[:, u[n]] = rng.integers(0, M, (16, L)) + 4096 * rng.integers(0, 16, (16, L))
def setup_inputs_crowd(rng):
    X = some(rng, M, (16, 64, 128)); B = some(rng, H, (160, 256)); x = np.minimum(some(rng, L, (128, 256)) + rng.integers(0, 64, (N, 8, 1, L)), 255)
    k = rng.integers(0, 17, (N, 8, 16, M)) * (rng.random((N, 8, 16, M)) < 0.3); fill = rng.choice(np.array([0.5, 1.0]), (N, 8, 1, M))
    E = 4096 * k + np.where(rng.random((N, 8, 16, M)) < fill, rng.integers(0, M, (N, 8, 16, M)), NONE)
    v = places(rng, rng.choice(np.array([1, 2, 3, 16]), (N, 8))); v[:, 0] = 0; v[:, 7] = M - 1
    o = rng.permutation(N); full(rng, X, B, E, x, v, int(o[0]), False); full(rng, X, B, E, x, v, int(o[1]), True)
    return pack(X, B, E, x, v, rng.integers(0, 16, (N, 8, 16, 2)))
def setup_inputs_ties(rng):
    X = 100 + rng.integers(0, 3, (N, 8, 16, M)); x = 100 + rng.integers(0, 3, (N, 8, 16, L)); B = rng.integers(0, 3, (N, 8, 16, H))
    c = rng.integers(0, M, (N, 8, 16, M)); c[:, ::2, 8:] = c[:, ::2, :8]
    E = 4096 * rng.integers(8, 15, c.shape) + np.where(rng.random(c.shape) < 0.8, c, NONE)
    v = places(rng, rng.choice(np.array([4, 16, 64, M]), (N, 8)))
    return pack(X, B, E, x, v, rng.integers(0, 16, (N, 8, 16, 2)))
def check_inputs(d):
    bad = []
    for k, lo, hi in (("nodes", 0, 255), ("book", 0, 255), ("kids", 0, 69631), ("cand", 0, 255), ("spot", 0, M - 1), ("wts", 0, 15)):
        a = np.asarray(d[k]).astype(np.float32)
        if not (np.min(a) >= lo and np.max(a) <= hi and np.all(a == np.floor(a))): bad.append("range of " + k)
    c = np.asarray(d["kids"]).astype(np.int64) & 4095
    if np.any((c >= M) & (c != NONE)): bad.append("children in kids")
    return bad
def reference(nodes, book, kids, cand, spot, wts):
    X = np.zeros((N, 8, 16, W), np.int64); X[..., :M] = nodes.astype(np.float32).astype(np.int64).reshape(N, 8, 16, M)
    E = np.full((N, 8, 16, W), NONE, np.int64); E[..., :M] = kids.astype(np.int64).reshape(N, 8, 16, M)
    B = book.astype(np.float32).astype(np.int64).reshape(N, 8, 16, H); w = wts.astype(np.float32).astype(np.int64).reshape(N, 8, 16, 2)
    xs = cand.astype(np.float32).astype(np.int64).reshape(N, 8, 16, L).copy(); vs = np.stack([gentries(a) for a in spot]).astype(np.int64)
    lane = np.arange(L); p = lane & 15; gr = np.arange(8)[:, None]
    for t in range(T):
        for r in range(N):
            x, v, q = xs[r], vs[r], (r + 1 + t % (N - 1)) % N
            ev = np.take_along_axis(E[r], v[:, None, :], 2)
            c = ev & 4095; thr = ev >> 12; filled = c != NONE
            xc = np.take_along_axis(X[r], np.where(filled, c, 0).reshape(8, 1, 16 * L), 2).reshape(8, 16, 16, L)
            dif = np.abs(x[:, :, None, :] - xc); fd = dif.reshape(8, 16, 16 * L)
            bc = np.take_along_axis(B[r], hashes(w[r], fd)[:, None, :], 2)
            s = np.add.reduce((bc >= fd).astype(np.int64), axis=1).reshape(8, 16, L)
            over = np.add.reduce((x[:, :, None, :] >= xc).astype(np.int64), axis=1)
            cap = filled & (over >= A) & (s > thr); stay = filled & ~cap
            go = stay[:, p, lane]
            best = np.argmax(np.where(stay, s, -1), axis=1)
            down = np.take_along_axis(c, best[:, None, :], 1)[:, 0]
            first = np.full((8, W), L); np.minimum.at(first, (gr, v), np.where(go, L, lane[None, :]))
            win = ~go & (first[gr, v] == lane[None, :]); wb = win[:, None, :]
            z = np.abs(np.take_along_axis(X[r], v[:, None, :], 2) - x)
            y = np.take_along_axis(B[q], hashes(w[q], z)[:, None, :], 2)
            n = M + L * t + lane
            X[r][:, :, M + L * t:M + L * t + L] = np.where(wb, x, 0)
            E[r][:, :, M + L * t:M + L * t + L] = np.where(wb & cap, c + 4096 * s, NONE)
            col = np.where(cap, NONE, ev); col[:, p, lane] = n[None, :] + 4096 * np.max(np.where(cap, s, 0), axis=1)
            gi, li = np.nonzero(win)
            E[r][gi, :, v[gi, li]] = col[gi, :, li]
            x = np.where(wb, np.abs(x - y), x)
            back = np.add.reduce(w[r][:, :, 0:1] * x, axis=1) & (R - 1)
            xs[r] = x; vs[r] = np.where(win, back, np.where(go, down, v))
    return {"ykids": E.reshape(N, 128, W).astype(np.float32), "ynodes": np.ascontiguousarray(X[..., M:]).reshape(N, 128, L * T).astype(np.float32).astype(BF),
            "ycand": xs.reshape(N, 128, L).astype(np.float32).astype(BF), "yspot": np.stack([gtable(a) for a in vs]).astype(np.float32)}

@@ -1,0 +1,702 @@
+import math
+from concourse.bass import DstId, RemoteDMATransfer
+from concourse.mybir import AluOpType as A, ActivationFunctionType as F
+
+N = 8
+M, L, NT = 2048, 192, 4
+W = M + L * NT
+BIGM = 1.5 * 2.0 ** 35
+LN32 = math.log(32.0)
+
+SCRATCH = {
+    "kI": ("sbuf", [128, 2048], "int32"), "Ef": ("sbuf", [128, 2816], "float32"),
+    "X": ("sbuf", [128, 4096], "bfloat16"), "bk3": ("sbuf", [128, 6144], "bfloat16"),
+    "x": ("sbuf", [128, 192], "bfloat16"), "sp": ("sbuf", [128, 12], "int32"), "wt": ("sbuf", [128, 2], "bfloat16"),
+    "ia": ("sbuf", [128, 192], "int32"), "ic": ("sbuf", [128, 192], "int32"), "ic2": ("sbuf", [128, 192], "int32"),
+    "ib": ("sbuf", [128, 128], "int32"), "dgi": ("sbuf", [128, 192], "int32"), "i8": ("sbuf", [128, 8], "int32"),
+    "p0": ("sbuf", [128, 1], "int32"), "p1": ("sbuf", [128, 1], "int32"), "p2": ("sbuf", [128, 1], "int32"),
+    "pm": ("sbuf", [128, 1], "float32"), "pb": ("sbuf", [128, 1], "float32"),
+    "nci": ("sbuf", [128, 768], "int32"), "NC": ("sbuf", [128, 768], "float16"),
+    "dli": ("sbuf", [128, 48], "int32"), "DL": ("sbuf", [128, 48], "float32"), "DLm": ("sbuf", [128, 48], "float32"),
+    "dgS": ("sbuf", [128, 192], "bfloat16"), "LT": ("sbuf", [128, 8, 16], "bfloat16"),
+    "NegI": ("sbuf", [128, 128], "bfloat16"), "NI4": ("sbuf", [128, 128], "bfloat16"),
+    "PI4": ("sbuf", [128, 128], "bfloat16"), "Idb": ("sbuf", [128, 128], "bfloat16"), "xc": ("sbuf", [128, 1024], "bfloat16"),
+    "Idh": ("sbuf", [128, 128], "float16"), "B16": ("sbuf", [128, 128], "bfloat16"),
+    "B16h": ("sbuf", [128, 128], "float16"), "B4h": ("sbuf", [128, 128], "float16"),
+    "BT": ("sbuf", [128, 128], "bfloat16"), "Tri": ("sbuf", [128, 128], "bfloat16"),
+    "tri0": ("sbuf", [128, 128], "bfloat16"), "G8": ("sbuf", [128, 8], "bfloat16"),
+    "Sm": ("sbuf", [128, 2048], "float16"), "RM": ("sbuf", [128, 192], "float32"),
+    "c88": ("sbuf", [128, 192], "float16"),
+    "PW1": ("sbuf", [128, 143], "bfloat16"), "PW2": ("sbuf", [128, 143], "bfloat16"), "P1s": ("sbuf", [128, 143], "bfloat16"),
+    "voff": ("sbuf", [128, 12], "uint16"), "soff": ("sbuf", [128, 12], "uint16"), "vm": ("sbuf", [128, 12], "float32"),
+    "vp1": ("sbuf", [128, 12], "float32"), "vmh": ("sbuf", [128, 12], "float16"), "vmd": ("sbuf", [128, 12], "float32"),
+    "bki": ("sbuf", [128, 12], "int32"), "bka": ("sbuf", [128, 12], "int32"), "bkf": ("sbuf", [128, 12], "float32"),
+    "bmv": ("sbuf", [128, 12], "float32"), "vlw": ("sbuf", [128, 12], "float32"), "ta": ("sbuf", [128, 12], "float32"),
+    "tb": ("sbuf", [128, 12], "float32"), "tc": ("sbuf", [128, 12], "float32"), "ts": ("sbuf", [128, 12], "float32"),
+    "ts2": ("sbuf", [128, 12], "float32"), "vfin": ("sbuf", [128, 12], "float32"),
+    "ev": ("sbuf", [128, 192], "int32"), "Ci": ("sbuf", [128, 192], "int32"), "offs": ("sbuf", [128, 192], "uint16"),
+    "xr": ("sbuf", [128, 2048], "bfloat16"), "diff": ("sbuf", [128, 3072], "bfloat16"),
+    "D": ("sbuf", [128, 3072], "bfloat16"), "sg": ("sbuf", [128, 3072], "bfloat16"), "cmp": ("sbuf", [128, 3072], "bfloat16"),
+    "zd": ("sbuf", [128, 192], "bfloat16"), "z": ("sbuf", [128, 192], "bfloat16"),
+    "hb": ("sbuf", [128, 512], "float32"), "sb": ("sbuf", [128, 512], "float32"), "t2": ("sbuf", [128, 512], "bfloat16"), "u1s": ("sbuf", [128, 256], "float32"),
+    "Pi": ("sbuf", [128, 256], "int32"), "Pd": ("sbuf", [128, 256], "int32"), "He": ("sbuf", [128, 256], "float32"),
+    "h": ("sbuf", [128, 192], "uint16"),
+    "Ki": ("sbuf", [128, 192], "int32"), "emp": ("sbuf", [128, 192], "bfloat16"), "edg": ("sbuf", [128, 192], "bfloat16"),
+    "K2": ("sbuf", [128, 192], "float32"), "Cf": ("sbuf", [128, 192], "float16"), "bigK": ("sbuf", [128, 192], "float32"),
+    "CN": ("sbuf", [128, 384], "bfloat16"), "WW": ("sbuf", [128, 384], "bfloat16"), "isb": ("sbuf", [128, 384], "bfloat16"),
+    "sel": ("sbuf", [128, 384], "bfloat16"), "pay": ("sbuf", [128, 384], "float16"),
+    "wdgw": ("sbuf", [128, 192], "bfloat16"), "gdg": ("sbuf", [128, 192], "float32"), "dn": ("sbuf", [128, 192], "float32"),
+    "sc1": ("sbuf", [128, 192], "float32"), "sc2": ("sbuf", [128, 192], "float32"), "sc3": ("sbuf", [128, 192], "float32"),
+    "cR": ("sbuf", [128, 192], "float32"), "val": ("sbuf", [128, 192], "float32"), "wdg": ("sbuf", [128, 192], "bfloat16"),
+    "q2": ("sbuf", [128, 192], "float32"), "capw": ("sbuf", [128, 192], "bfloat16"), "q3": ("sbuf", [128, 192], "float32"),
+    "EQ": ("sbuf", [128, 12, 192], "bfloat16"), "xy": ("sbuf", [128, 192], "bfloat16"), "xw": ("sbuf", [128, 192], "bfloat16"),
+    "dx": ("sbuf", [128, 192], "bfloat16"),
+    "U0": ("psum", [128, 512], "float32"), "U1": ("psum", [128, 512], "float32"), "O": ("psum", [128, 512], "float32"),
+    "S0": ("psum", [128, 512], "float32"), "S1": ("psum", [128, 512], "float32"), "TB": ("psum", [128, 512], "float32"),
+    "VP": ("psum", [128, 512], "float32"), "CB": ("psum", [128, 512], "float32"),
+}
+SCRATCH["FP"] = ("sbuf", [128, 8 * 144], "bfloat16")
+for _n, _w, _d in (("wf", 2, "bfloat16"), ("zq", 12, "uint16"), ("qi", 12, "uint16"), ("yo", 192, "bfloat16"), ("yi", 192, "bfloat16")):
+    SCRATCH[_n] = ("sbuf", [128, NT * _w], _d)
+PSUM = [n for n in SCRATCH if SCRATCH[n][0] == "psum"]
+NDMA = 16
+SEMAPHORES = ["sV", "sS", "sP", "sG", "lsem", "wa"] + ["qa%d" % t for t in range(NT)] + ["ra%d" % t for t in range(NT)] + ["d%d" % i for i in range(NDMA)]
+
+
+def tracker(g, T):
+    eng = {"V": g.vector, "S": g.scalar, "P": g.tensor, "G": g, "Y": g.sync}
+    know = {q: {} for q in eng}
+    cnt = {q: 0 for q in eng}
+    wr, rd, bank, used = {}, {}, {}, [0]
+
+    def waits(q, ops):
+        k = know[q]
+        ops = [o for o in ops if k.get(o[0], 0) < o[1]]
+        ops.sort(key=lambda o: -len(o[2]))
+        best = {}
+        for o in ops:
+            if o[0] not in best or best[o[0]][1] < o[1]:
+                best[o[0]] = o
+        ops = list(best.values())
+        keep = []
+        for o in ops:
+            if not any(p is not o and p[2].get(o[0], 0) >= o[1] for p in ops):
+                keep.append(o)
+        for o in keep:
+            eng[q].wait_ge(T.sem[o[0]], o[1])
+        for o in keep:
+            for s, v in o[2].items():
+                if k.get(s, 0) < v:
+                    k[s] = v
+
+    def deps(q, reads, writes, dma):
+        out = []
+        for n, lo, hi in reads:
+            out += [o for a, b, o in wr.get(n, []) if a < hi and lo < b]
+        for n, lo, hi in writes:
+            for a, b, o in wr.get(n, []):
+                if a < hi and lo < b and not (o[3] == q == "P"):
+                    out.append(o)
+            for a, b, o in rd.get(n, []):
+                if a < hi and lo < b and (o[3] != q or dma):
+                    out.append(o)
+        for n in set([r[0] for r in reads + writes]):
+            if n in PSUM:
+                out += [o for p, o in bank.get(n, {}).items() if p != q]
+        if q == "P":
+            out = [o for o in out if o[3] != "P"]
+        return out
+
+    def note(op, reads, writes, q):
+        for n, lo, hi in writes:
+            wr[n] = [e for e in wr.get(n, []) if not (lo <= e[0] and e[1] <= hi)] + [(lo, hi, op)]
+            rd[n] = [e for e in rd.get(n, []) if not (lo <= e[0] and e[1] <= hi)]
+        for n, lo, hi in reads:
+            old = [e for e in rd.get(n, []) if not (lo <= e[0] and e[1] <= hi and e[2][3] == q and op[4] == 0 and e[2][4] == 0)]
+            rd[n] = old + [(lo, hi, op)]
+        for n in set([r[0] for r in reads + writes]):
+            if n in PSUM:
+                bank.setdefault(n, {})[q] = op
+
+    def emit(q, call, reads, writes, dma=False):
+        waits(q, deps(q, reads, writes, dma))
+        ins = call(eng[q])
+        if dma:
+            s, v = "d%d" % used[0], 16
+            used[0] += 1
+        else:
+            cnt[q] += 1
+            s, v = "s" + q, cnt[q]
+        ins.then_inc(T.sem[s], 16 if dma else 1)
+        clk = dict(know[q])
+        clk[s] = v
+        note((s, v, clk, "d" if dma else q, 1 if dma else 0), reads, writes, q)
+
+    def arrive(sem, val, name, lo, hi):
+        note((sem, val, {sem: val}, "X", 1), [], [(name, lo, hi)], "X")
+
+    def before(q, reads):
+        waits(q, deps(q, reads, [], True))
+
+    def finish():
+        for q in eng:
+            if cnt[q]:
+                g.wait_ge(T.sem["s" + q], cnt[q])
+        for i in range(used[0]):
+            g.wait_ge(T.sem["d%d" % i], 16)
+    return emit, arrive, before, finish
+
+
+WAKE, SELF = 0.10, 0.10
+
+
+def schedule(plan):
+    n = len(plan)
+    pred = [{} for _ in range(n)]
+    succ = [{} for _ in range(n)]
+    wr, rd = {}, {}
+
+    def edge(a, b, lat):
+        if a != b and pred[b].get(a, -1.0) < lat:
+            pred[b][a] = lat
+            succ[a][b] = lat
+    for i, (q, _c, reads, writes, kind, _d, after) in enumerate(plan):
+        for j in after:
+            edge(j, i, 0.0)
+        for b, lo, hi in reads:
+            for x, y, j in wr.get(b, []):
+                if x < hi and lo < y:
+                    edge(j, i, WAKE if plan[j][0] != q or kind == "d" else 0.0 if q == "P" else SELF)
+        for b, lo, hi in writes:
+            for x, y, j in wr.get(b, []) + rd.get(b, []):
+                if x < hi and lo < y:
+                    edge(j, i, WAKE if plan[j][0] != q else 0.0)
+        for b, lo, hi in writes:
+            wr[b] = [e for e in wr.get(b, []) if not (lo <= e[0] and e[1] <= hi)] + [(lo, hi, i)]
+            rd[b] = [e for e in rd.get(b, []) if not (lo <= e[0] and e[1] <= hi)]
+        for b, lo, hi in reads:
+            rd.setdefault(b, []).append((lo, hi, i))
+    left = [len(p) for p in pred]
+    end = [0.0] * n
+    early = [0.0] * n
+    free, bank, dfree = {}, {}, 0.0
+    banks = [sorted(set(b for b, _l, _h in p[2] + p[3] if b in PSUM)) for p in plan]
+    ready = [i for i in range(n) if left[i] == 0]
+    order = []
+    while ready:
+        best = None
+        for i in ready:
+            q = plan[i][0]
+            t = max(early[i], free.get(q, 0.0)) if q != "X" else early[i]
+            for b in banks[i]:
+                for q2, e in bank.get(b, {}).items():
+                    if q2 != q and e + WAKE > t:
+                        t = e + WAKE
+            key = (round(t / SLOT), i)
+            if best is None or key < best[0]:
+                best = (key, i, t)
+        _k, i, t = best
+        ready.remove(i)
+        order.append(i)
+        q, kind, d = plan[i][0], plan[i][4], plan[i][5]
+        if kind == "d":
+            free[q] = t + 0.1
+            dfree = max(dfree, t + 1.0) + d
+            end[i] = dfree + 1.0
+        else:
+            end[i] = t + d
+            free[q] = end[i]
+        for b in banks[i]:
+            bank.setdefault(b, {})[q] = end[i]
+        for j, lat in succ[i].items():
+            early[j] = max(early[j], end[i] + lat)
+            left[j] -= 1
+            if left[j] == 0:
+                ready.append(j)
+    return order
+
+
+SLOT = 0.02
+ORDER = {}
+
+
+def rank_program(g, core, T, topo):
+    r = T.rank_of(core)
+    if r is None:
+        return
+    emit_now, arrive_now, before, finish = tracker(g, T)
+    plan = []
+
+    def emit(q, call, reads, writes, dma=False, dur=0.06):
+        plan.append((q, [call], reads, writes, "d" if dma else "c", dur, []))
+
+    def cols(x):
+        return x[2] if len(x) > 2 else x[1][0][2] - x[1][0][1]
+
+    def dt_of(x):
+        return SCRATCH.get(x[1][0][0], ("sbuf", 0, "bfloat16"))[2]
+
+    def in_psum(x):
+        return x[1][0][0] in PSUM
+
+    CYC = 0.00085
+
+    def time_of(out, a, b=None):
+        if len(a) > 3:
+            return 0.06 + 1.56 * CYC * cols(out)
+        if len(out) > 3:
+            return 0.06 + 3.8 * CYC * cols(a)
+        n = cols(out)
+        if b is not None:
+            f = 1.0 if in_psum(a) or in_psum(b) else 2.0
+        else:
+            f = 0.5 if not in_psum(a) and not in_psum(out) and dt_of(a) in TWO and dt_of(out) in TWO else 1.0
+        return CYC * max(64, f * n)
+    TWO = ("bfloat16", "float16", "uint16")
+    group = []
+    width = {n: (SCRATCH[n][1][1] if len(SCRATCH[n][1]) == 2 else SCRATCH[n][1][1] * SCRATCH[n][1][2]) for n in SCRATCH}
+
+    def o(n, lo=0, hi=None, step=1):
+        hi = width[n] if hi is None else hi
+        return (T[n][:, lo:hi] if step == 1 else T[n][:, lo:hi:step], [(n, lo, hi)], (hi - lo + step - 1) // step)
+
+    def ind(n, lo, hi, off):
+        return (T[n][:, lo:hi].indirect(off[0]), [(n, lo, hi)] + off[1], 16 * off[2], "indirect")
+
+    def sca(s):
+        return (s[0], s[1]) if isinstance(s, tuple) else (s, [])
+
+    def tt(out, a, b, op):
+        emit("V", lambda e: e.tensor_tensor(out[0], a[0], b[0], op), a[1] + b[1], out[1], dur=time_of(out, a, b))
+
+    def ts(out, a, s1, op0, s2=None, op1=None):
+        s1 = sca(s1)
+        if op1 is None:
+            emit("V", lambda e: e.tensor_scalar(out[0], a[0], s1[0], None, op0), a[1] + s1[1], out[1], dur=time_of(out, a))
+        else:
+            emit("V", lambda e: e.tensor_scalar(out[0], a[0], s1[0], s2, op0, op1), a[1] + s1[1], out[1], dur=time_of(out, a))
+
+    def cp(out, a):
+        emit("V", lambda e: e.tensor_copy(out[0], a[0]), a[1] + out[1][1:], out[1][:1], dur=time_of(out, a))
+
+    def ms(out, c):
+        emit("V", lambda e: e.memset(out[0], c), [], out[1], dur=CYC * cols(out))
+
+    def scan(out, a, b):
+        emit("V", lambda e: e.tensor_tensor_scan(out[0], a[0], b[0], 0.0, A.mult, A.add), a[1] + b[1], out[1], dur=CYC * cols(out))
+
+    def act(out, a, func, scale=1.0, bias=0.0):
+        emit("S", lambda e: e.activation(out[0], a[0], func, bias=bias, scale=scale), a[1], out[1],
+             dur=0.065 + CYC * cols(a) * (1.56 if len(a) > 3 else 1.0))
+
+    def mm(out, lhsT, rhs, start, stop, whole=None, cut=False):
+        group.append((lambda e: e.matmul(out[0], lhsT[0], rhs[0], start, stop), lhsT[1] + rhs[1], out[1] + ([(whole, 0, 512)] if whole else []),
+                      0.0007 * max(64, cols(rhs)) * (4 if dt_of(rhs) == "float32" else 1)))
+        if stop or cut:
+            plan.append(("P", [c[0] for c in group], sorted(set(x for c in group for x in c[1])), sorted(set(x for c in group for x in c[2])),
+                         "c", sum(c[3] for c in group), []))
+            del group[:]
+
+    def iota(n, pattern, base, cm):
+        b = o(n)
+        emit("G", lambda e: e.iota(b[0], pattern, base, cm), [], b[1], dur=0.15 + 2 * CYC * cols(b))
+
+    def load(q, name, lo, hi, src):
+        b = o(name, lo, hi)
+        emit(q, lambda e: e.dma_start(b[0], src), [], b[1], dma=True, dur=0.0013 * cols(b) * (1 if dt_of(b) in TWO else 2))
+
+    def store(q, dst, b):
+        emit(q, lambda e: e.dma_start(dst, b[0]), b[1], [], dma=True, dur=0.0013 * cols(b) * (1 if dt_of(b) in TWO else 2))
+
+    load("S", "wt", 0, 2, T.wts[:, :])
+    load("Y", "sp", 0, 12, T.spot[:, :])
+    load("Y", "kI", 0, 2048, T.kids[:, :])
+    load("S", "x", 0, 192, T.cand[:, :])
+    load("Y", "X", 0, 2048, T.nodes[:, :])
+    for j in range(3):
+        load("Y", "bk3", 2048 * j, 2048 * j + 2048, T.book[:, :])
+
+    iota("p0", [[0, 1]], 0, 1)
+    iota("ia", [[1, 192]], 1024, -1)
+    iota("ic", [[1, 192]], 0, 0)
+    iota("i8", [[1, 8]], 0, 0)
+    iota("dli", [[16, 48]], 2048, 0)
+    iota("nci", [[1, 768]], -2047, 0)
+
+    allto = [T.cores[(r - 1 - t) % N] for t in range(NT)]
+    common = [e for e in topo.engines(core, allto[0]) if all(e in topo.engines(core, c) for c in allto)][:8]
+    wmask = sum(1 << e for e in common)
+    lcount = [0]
+
+    def send_weights():
+        g.remote_dma_fused([RemoteDMATransfer(
+            dst_ids=[DstId(rid=topo.addr(c)[0], pnc=topo.addr(c)[1]) for c in allto], dma_engine_mask=wmask,
+            remote_sem=T.sem.wa, srcs=[T.wt[:, :]], dsts=[T.wf[:, 2 * t:2 * t + 2] for t in range(NT)])], local_sem=T.sem.lsem)
+        lcount[0] += len(common)
+
+    def arrive(sem, val, name, lo, hi, lat):
+        plan.append(("X", [lambda: arrive_now(sem, val, name, lo, hi)], [], [(name, lo, hi)], "x", lat, [sends[-1]]))
+
+    sends = [len(plan)]
+    plan.append(("G", [send_weights], [("wt", 0, 2)], [], "s", 1.0, []))
+    arrive("wa", len(common) * NT, "wf", 0, 2 * NT, 4.0)
+
+    def send(dst, out_n, in_n, lo, hi, sem):
+        eng = topo.engines(core, dst)[:8]
+        rid, pid, _s = topo.addr(dst)
+
+        def call():
+            g.remote_dma(T[out_n][:, lo:hi], T[in_n][:, lo:hi], T.sem[sem], T.sem.lsem, pid, rid, sum(1 << e for e in eng))
+            lcount[0] += len(eng)
+        sends.append(len(plan))
+        plan.append(("G", [call], [(in_n, lo, hi)], [], "s", 1.0, []))
+
+    ms(o("X", 2048, 4080), 0.0)
+    ms(o("X", 4080, 4096), 512.0)
+    ms(o("Ef", 2048, 2816), 4095.0)
+    for n in ("PW1", "PW2", "P1s", "FP"):
+        ms(o(n), 0.0)
+    cp(o("voff"), o("sp"))
+    ts(o("vm"), o("sp"), -1408.0, A.add)
+    ts(o("vp1"), o("sp"), 1.0, A.add)
+    cp(o("vmh"), o("vm"))
+    ts(o("p1"), o("p0"), 15, A.bitwise_and)
+    cp(o("pm"), o("p1"))
+    ts(o("p2"), o("p0"), 4, A.arith_shift_right)
+    cp(o("pb"), o("p2"))
+    ts(o("dgi"), o("ia"), 15, A.bitwise_and)
+    ts(o("dgS"), o("dgi"), 0.0, A.is_equal)
+    dgP = lambda lo, hi: o("VP", lo, hi)
+    ts(o("VP", 0, 192), o("dgi"), 0.0, A.is_equal)
+    ts(o("NegI"), o("ia", 0, 128), 1024.0, A.is_equal, -1.0, A.mult)
+    ts(o("NI4"), o("ia", 0, 128), 1024.0, A.is_equal, -1.0 / 4096, A.mult)
+    ts(o("PI4"), o("ia", 0, 128), 1024.0, A.is_equal, 1.0 / 4096, A.mult)
+    ts(o("Idb"), o("ia", 0, 128), 1024.0, A.is_equal)
+    ts(o("Idh"), o("ia", 0, 128), 1024.0, A.is_equal)
+    ts(o("ib"), o("ic", 0, 128), 4, A.arith_shift_right)
+    ts(o("B16"), o("ib"), o("pb"), A.is_equal)
+    cp(o("B16h"), o("B16"))
+    ts(o("B4h"), o("B16"), 4096.0, A.mult)
+    ts(o("BT"), o("B16"), 3.0 / 64, A.mult)
+    ts(o("tri0"), o("ia", 0, 128), 1024.0, A.is_gt)
+    tt(o("Tri"), o("tri0"), o("B16"), A.mult)
+    ts(o("G8"), o("i8"), o("pb"), A.is_equal)
+    ts(o("P1s", 15, 143, 16), o("G8"), 1.0, A.mult)
+    ts(o("ic2"), o("ic"), 15, A.bitwise_and)
+    ts(o("RM"), o("ic2"), 0.0, A.is_gt)
+    for e_ in range(8):
+        ts((T.LT[:, e_, :], [("LT", 16 * e_, 16 * e_ + 16)]), o("ic", 0, 16), o("pm"), A.is_gt)
+    ts(o("c88"), o("RM"), 0.0, A.mult, 88.0625, A.add)
+    for m in range(16):
+        ts(o("Sm", 128 * m, 128 * m + 128), o("B16h"), o("dgS", m, m + 1), A.mult)
+    ts(o("DL"), o("dli"), o("pm"), A.add)
+    ts(o("DLm"), o("DL"), -1408.0, A.add)
+    cp(o("NC"), o("nci"))
+    ts(o("PW1", 15, 143, 16), o("G8"), o("wt", 0, 1), A.mult)
+    ts(o("PW2", 15, 143, 16), o("G8"), o("wt", 1, 2), A.mult)
+
+    def window(n, k, base=0):
+        return o(n, base + 15 - k, base + 143 - k)
+
+    def repeat():
+        for k in range(16):
+            act((T.xr[:, k:2048:16], [("xr%d" % k, 0, 2048)]), o("x", 0, 128), F.Copy)
+
+    repeat()
+
+    CH = ((0, 64), (64, 128), (128, 192))
+    UB = ("U0", "U1", "U0")
+    deferred = []
+
+    def gather_slots(t, lo, hi):
+        tab = ("kI", 0, 2048) if t == 0 else ("Ef", 0, W)
+        cp(o("ev", lo, hi), ind(tab[0], tab[1], tab[2], o("voff", lo // 16, hi // 16)))
+        ts(o("Ci", lo, hi), o("ev", lo, hi), 4095, A.bitwise_and)
+        cp(o("offs", lo, hi), o("Ci", lo, hi))
+
+    def hash_mod(U, n, w):
+        c = (128 * w, 128 * w + 2 * n)
+        act(o("sb", *c), o(U, 0, 2 * n), F.Identity, bias=-2047.5)
+        act(o("hb", *c), o("sb", *c), F.Identity, bias=BIGM)
+        act(o("t2", *c), o("hb", *c), F.Identity, bias=-BIGM)
+
+    def hash_end(U, n, w, out):
+        c = (64 * w, 64 * w + n)
+        u2 = o(U, n, 2 * n)
+        tt(u2, u2, o("t2", 128 * w + n, 128 * w + 2 * n), A.subtract)
+        tt(o("u1s", *c), o(U, 0, n), o("t2", 128 * w, 128 * w + n), A.subtract)
+        tt(o("Pi", *c), o("u1s", *c), u2, A.mult)
+        ts(o("Pd", *c), o("Pi", *c), 5, A.arith_shift_right, 2047, A.bitwise_and)
+        tt(o("He", *c), o("Pd", *c), u2, A.add)
+        cp(out, o("He", *c))
+
+    for t in range(NT):
+        last = t == NT - 1
+        b = T.cores[(r + 1 + t) % N]
+        asker = T.cores[(r - 1 - t) % N]
+
+        def XG(c):
+            lo, hi = CH[c]
+            dv = o("diff", 16 * lo, 16 * hi)
+            xg = ind("X", 0, 4096, o("offs", lo, hi))
+            xv = (T.xr[:, 16 * lo:16 * hi], [("xr%d" % k, 16 * lo, 16 * hi) for k in range(16)])
+            tt(dv, xg, xv, A.subtract)
+            act(o("D", 16 * lo, 16 * hi), dv, F.Abs)
+
+        def usum(c, j):
+            lo, hi = CH[c]
+            U = UB[c]
+            for k in range(16):
+                mm(o(U, 64 * j, 64 * j + 64), window("PW%d" % (j + 1), k), o("D", 16 * lo + k, 16 * hi, 16), k == 0, k == 15)
+
+        def BG(c):
+            lo, hi = CH[c]
+            tt(o("cmp", 16 * lo, 16 * hi), ind("bk3", 0, 6144, o("h", lo, hi)), o("D", 16 * lo, 16 * hi), A.is_ge)
+
+        def sign(c):
+            lo, hi = CH[c]
+            if c == 2:
+                for hf in range(2):
+                    act(o("sg", 2048 + 512 * hf, 2560 + 512 * hf), o(("TB", "S1")[hf]), F.Sign, scale=-1.0, bias=0.5)
+            else:
+                ts(o("sg", 16 * lo, 16 * hi), o("diff", 16 * lo, 16 * hi), 0.0, A.is_le)
+
+        def over(c):
+            lo, hi = CH[c]
+            for k in range(16):
+                mm(o("O", lo, hi), window("P1s", k), o("sg", 16 * lo + k, 16 * hi, 16), k == 0, k == 15)
+
+        def ssum(c):
+            lo, hi = CH[c]
+            so = o("S0", lo, hi) if c < 2 else o("S1", 0, 64)
+            mm(so, o("PI4"), o("emp", lo, hi), True, False)
+            mm(so, o("NI4"), o("edg", lo, hi), False, False)
+            for k in range(16):
+                mm(so, window("P1s", k), o("cmp", 16 * lo + k, 16 * hi, 16), False, k == 15)
+
+        gather_slots(t, 0, 64)
+        if t == 0:
+            gather_slots(t, 64, 192)
+            cp(o("Ef", 0, 2048), o("kI"))
+            for j in range(2 * NT):
+                ts(o("FP", 144 * j + 15, 144 * j + 143, 16), o("G8"), o("wf", j, j + 1), A.mult)
+        tt(o("zd"), ind("X", 0, 4096, o("voff")), o("x"), A.subtract)
+        act(o("z"), o("zd"), F.Abs)
+        if t > 0:
+            gather_slots(t, 64, 192)
+        act(o("xc"), ind("X", 0, 4096, o("offs", 128, 192)), F.Copy)
+        for j in range(2):
+            for m in range(16):
+                mm(o("U1", 12 * j, 12 * j + 12), window("FP", m, 144 * (2 * t + j)), o("z", m, 192, 16), m == 0, m == 15)
+        XG(0)
+        for f in deferred:
+            f()
+        del deferred[:]
+        usum(0, 0)
+        hash_mod("U1", 12, 3)
+        usum(0, 1)
+        XG(1)
+        ts(o("emp"), o("Ci"), 4095.0, A.is_equal, -4096.0, A.mult)
+        ts(o("Ki"), o("ev"), 12, A.arith_shift_right)
+        hash_end("U1", 12, 3, o("zq", 12 * t, 12 * t + 12))
+        send(b, "qi", "zq", 12 * t, 12 * t + 12, "qa%d" % t)
+        arrive("qa%d" % t, len(topo.engines(asker, core)[:8]), "qi", 12 * t, 12 * t + 12, 3.5)
+        for hf in range(2):
+            bank = ("TB", "S1")[hf]
+            mm(o(bank), o("Idb"), o("xc", 512 * hf, 512 * hf + 512), True, False)
+            for k in range(16):
+                mm(o(bank, k, 512, 16), o("NegI"), o("x", 128 + 32 * hf, 160 + 32 * hf), False, k == 15)
+        hash_mod("U0", 64, 0)
+        for hf in range(2):
+            act(o("D", 2048 + 512 * hf, 2560 + 512 * hf), o(("TB", "S1")[hf]), F.Abs)
+        usum(1, 0)
+        usum(1, 1)
+        sign(0)
+        tt(o("edg"), dgP(0, 192), o("emp"), A.mult)
+        ts(o("Cf"), o("Ci"), -1408.0, A.add)
+        tt(o("K2"), o("Ki"), o("edg"), A.add)
+        hash_end("U0", 64, 0, o("h", 0, 64))
+        BG(0)
+        hash_mod("U1", 64, 1)
+        usum(2, 0)
+        usum(2, 1)
+        sign(2)
+        ts(o("VP", 256, 448), o("ev"), -1.0, A.mult, 4095.0, A.add)
+        hash_end("U1", 64, 1, o("h", 64, 128))
+        BG(1)
+        mm(o("CB", 0, 192), o("B16h"), o("c88"), True, False)
+        for m in range(16):
+            mm(o("CB", m, 192, 16), o("Sm", 128 * m, 128 * m + 128), o("vmh"), False, m == 15)
+        over(0)
+        hash_mod("U0", 64, 2)
+        ssum(0)
+        sign(1)
+        over(1)
+        act(o("yo", L * t, L * t + L), ind("bk3", 0, 6144, o("qi", 12 * t, 12 * t + 12)), F.Copy)
+        send(asker, "yi", "yo", L * t, L * t + L, "ra%d" % t)
+        arrive("ra%d" % t, len(topo.engines(b, core)[:8]), "yi", L * t, L * t + L, 4.5)
+        act(o("O", 192, 320), o("O", 0, 128), F.Relu, scale=-128.0, bias=1216.0)
+        hash_end("U0", 64, 2, o("h", 128, 192))
+        BG(2)
+        ssum(1)
+        tt(o("vmd"), o("vm"), o("DLm", 12 * t, 12 * t + 12), A.subtract)
+
+        def batch(lo, hi, SB, t=t, last=last):
+            n = hi - lo
+            c0, c1 = lo // 16, hi // 16
+            a, e = 2 * lo, 2 * lo + n
+            z_ = 2 * hi
+            T0, L0, W0 = (0, 256, 256) if lo == 0 else (384, 384, 0)
+            S = o(SB, 0, n)
+            EX = o(SB, n, 2 * n)
+            Q1 = o(SB, 2 * n, 3 * n)
+            last_lane = lambda nm: o(nm, lo + 15, hi, 16)
+            lst = lambda nm: o(nm, c0, c1)
+
+            def d1():
+                act(EX, S, F.Exp, scale=LN32)
+                act(Q1, S, F.Identity, scale=4096.0, bias=-4095.0)
+                tt(o("bigK", lo, hi), o("O", 192 + lo, 192 + hi), o("K2", lo, hi), A.add)
+                tt(o("CN", e, z_), S, o("bigK", lo, hi), A.is_gt)
+                tt(o("CN", a, e), S, o("bigK", lo, hi), A.is_le)
+                tt(o("WW", a, e), EX, o("CN", a, e), A.mult)
+                tt(o("WW", e, z_), EX, o("CN", e, z_), A.mult)
+                mm(o("TB", T0, T0 + 2 * n), o("BT"), o("WW", a, z_), True, True)
+
+            def d2():
+                tt(o("wdgw", lo, hi), dgP(lo, hi), o("CN", e, z_), A.mult)
+                scan(o("sc1", lo, hi), o("RM", lo, hi), o("wdgw", lo, hi))
+                tt(o("isb", a, z_), o("WW", a, z_), o("TB", T0, T0 + 2 * n), A.is_gt)
+                mm(o("TB", L0, L0 + 2 * n), o("Tri"), o("isb", a, z_), True, True)
+
+            def d3():
+                tt(lst("vlw"), last_lane("sc1"), lst("vp1"), A.mult)
+                tt(o("gdg", lo, hi), dgP(lo, hi), o("CN", a, e), A.mult)
+                tt(Q1, Q1, o("Ci", lo, hi), A.add)
+                tt(o("sel", a, z_), o("isb", a, z_), o("TB", L0, L0 + 2 * n), A.is_gt)
+                tt(o("pay", e, z_), S, o("sel", e, z_), A.mult)
+                tt(o("pay", a, e), o("sel", a, e), o("Cf", lo, hi), A.mult)
+                mm(o("TB", T0 + n, T0 + 2 * n), o("Idh"), o("NC", L * t + lo, L * t + hi), True, False)
+                mm(o("TB", T0 + n, T0 + 2 * n), o("B4h"), o("pay", e, z_), False, True)
+                mm(o("TB", T0, T0 + n), o("B16h"), o("pay", a, e), True, True)
+
+            def d4():
+                for c in range(c0, c1):
+                    ts((T.EQ[:, c, 0:L - 16 * c], [("EQ", L * c, L * c + L - 16 * c)]), o("CB", 16 * c, L), o("vlw", c, c + 1), A.is_equal)
+                eqd = (T.EQ[:, c0:c1, 0:16], [("EQ", L * c0, L * c1)], 16 * (c1 - c0))
+                tt(eqd, eqd, (T.LT[:, 0:c1 - c0, :], [("LT", 0, 16 * (c1 - c0))]), A.mult)
+
+                def count(cs, x0, x1, first, final):
+                    for c in cs:
+                        s = max(x0, 16 * c)
+                        mm(o("CB", 192 + s, 192 + x1), o("B16"), (T.EQ[:, c, s - 16 * c:x1 - 16 * c], [("EQ", L * c, L * c + L)], x1 - s),
+                           first and c == cs[0], final and c == cs[-1])
+                if lo == 0:
+                    count(list(range(8)), 0, 128, True, True)
+                else:
+                    count(list(range(12)), 128, 192, True, True)
+
+            def d5():
+                tt(o("VP", 256 + lo, 256 + hi), o("VP", 256 + lo, 256 + hi), o("CN", e, z_), A.mult)
+                tt(o("VP", 256 + lo, 256 + hi), o("VP", 256 + lo, 256 + hi), o("ev", lo, hi), A.add)
+                tt(o("wdg", lo, hi), o("wdgw", lo, hi), o("CB", 192 + lo, 192 + hi), A.is_gt)
+                mm(o("TB", W0, W0 + n), o("B16"), o("wdg", lo, hi), True, True)
+                scan(o("sc3", lo, hi), o("RM", lo, hi), o("wdg", lo, hi))
+                tt(lst("ts"), last_lane("sc3"), lst("vmd"), A.mult)
+                tt(o("dn", lo, hi), o("TB", T0, T0 + n), o("gdg", lo, hi), A.mult)
+                tt(lst("ts2"), lst("ts"), o("DL", 12 * t + c0, 12 * t + c1), A.add)
+                tt(o("cR", lo, hi), o("TB", T0 + n, T0 + 2 * n), o("dgS", lo, hi), A.mult)
+                cp(lst("soff"), lst("ts2"))
+                scan(o("sc2", lo, hi), o("RM", lo, hi), o("dn", lo, hi))
+                tt(o("val", lo, hi), o("VP", 256 + lo, 256 + hi), o("cR", lo, hi), A.add)
+                tt(lst("ta"), last_lane("sc1"), lst("vm"), A.mult)
+                cp(ind("Ef", 0, W, lst("soff")), o("val", lo, hi))
+                tt(lst("tb"), lst("ta"), last_lane("sc2"), A.add)
+
+            def d8():
+                tt(lst("tc"), last_lane("sc3"), lst("bmv"), A.mult)
+                tt(lst("vm"), lst("tb"), lst("tc"), A.add)
+                if last:
+                    ts(lst("vfin"), lst("vm"), 1408.0, A.add)
+                else:
+                    ts(lst("voff"), lst("vm"), 1408.0, A.add)
+
+            def d6():
+                WR = o("TB", W0, W0 + n)
+                nl = M + L * t
+                tt(o("VP", 256 + lo, 256 + hi), WR, o("dx", lo, hi), A.mult)
+                tt(o("X", nl + lo, nl + hi), WR, o("x", lo, hi), A.mult)
+                tt(o("x", lo, hi), o("VP", 256 + lo, 256 + hi), o("x", lo, hi), A.add)
+                if not last and lo == 0:
+                    repeat()
+
+            def d7():
+                nl = M + L * t
+                tt(o("capw", lo, hi), o("TB", W0, W0 + n), o("CN", e, z_), A.mult)
+                tt(o("q3", lo, hi), Q1, o("capw", lo, hi), A.mult)
+                act(o("Ef", nl + lo, nl + hi), o("q3", lo, hi), F.Identity, bias=4095.0)
+
+            def d9():
+                cp(lst("vmh"), lst("vm"))
+                ts(lst("vp1"), lst("vm"), 1409.0, A.add)
+            return d1, d2, d3, d4, d5, d6, d7, d8, d9
+
+        AB = batch(0, 128, "S0")
+        C = batch(128, 192, "S1")
+        ssum(2)
+        AB[0]()
+        over(2)
+        act(o("O", 320, 384), o("O", 128, 192), F.Relu, scale=-64.0, bias=192.0)
+        AB[1]()
+        AB[2]()
+        C[0]()
+        mm(o("O", 0, 192), o("Idb"), o("x"), True, False)
+        mm(o("O", 0, 192), o("NegI"), o("yi", L * t, L * t + L), False, True)
+        act(o("xw"), o("O", 0, 192), F.Abs)
+        AB[3]()
+        C[1]()
+        mm(o("O", 0, 192), o("Idb"), o("xw"), True, False)
+        mm(o("O", 0, 192), o("NegI"), o("x"), False, True)
+        act(o("dx"), o("O", 0, 192), F.Copy)
+        for m in range(16):
+            mm(o("O", 384, 396), window("PW1", m), o("xw", m, 192, 16), m == 0, m == 15)
+        C[2]()
+        AB[4]()
+        cp(o("bki"), o("O", 384, 396))
+        ts(o("bka"), o("bki"), 1023, A.bitwise_and)
+        C[3]()
+        ts(o("bkf"), o("bka"), 1.0, A.add)
+        AB[6]()
+        tt(o("bmv"), o("bkf"), o("vp1"), A.subtract)
+        AB[5]()
+        AB[7]()
+        C[4]()
+        C[7]()
+        C[5]()
+        if not last:
+            AB[8]()
+        if last:
+            store("Y", T.ykids[:, 0:W - L], o("Ef", 0, W - L))
+            C[6]()
+            store("S", T.ykids[:, W - L:W], o("Ef", W - L, W))
+            store("Y", T.ynodes[:, :], o("X", M, W))
+            store("S", T.ycand[:, :], o("x"))
+            store("Y", T.yspot[:, :], o("vfin"))
+        else:
+            deferred.extend((C[8], C[6]))
+
+    if "order" not in ORDER:
+        ORDER["order"] = schedule(plan)
+    for i in ORDER["order"]:
+        q, calls, reads, writes, kind, _d, _a = plan[i]
+        if kind == "x":
+            calls[0]()
+        elif kind == "s":
+            before("G", reads)
+            calls[0]()
+        else:
+            for c in calls[:-1]:
+                emit_now(q, c, reads, writes)
+            emit_now(q, calls[-1], reads, writes, dma=kind == "d")
+    finish()
+    g.wait_ge(T.sem.lsem, lcount[0])

@@ -5,60 +5,44 @@ from concourse.mybir import AluOpType as A, ActivationFunctionType as F
 N = 8
 M, L, NT = 2048, 192, 4
 W = M + L * NT
-BIGM = 1.5 * 2.0 ** 35
+PAD = 16
+BIG = 2.0 ** 18
+C12, C10 = 1.5 * 2.0 ** 19, 1.5 * 2.0 ** 17
 LN32 = math.log(32.0)
+LNB = math.log(1.8)
+CFG = {"path": "VSS", "sign": "VVS", "piece": 2, "xr": "S", "G": "SS", "xn": "SS", "delta": 0.12, "rounds": 1, "ev": ((0, 64), (64, 128), (128, 192)), "tol": 0.1, "bg": 2, "step": 16.0,
+       "due": {"offs0": 0.8, "offs64": 1.0, "D0": 3.7, "D1": 5.0, "D2": 7.9, "zq": 4.0, "yi": 8.5, "early": 5.0, "cmp0": 7.7, "cmp1": 9.4, "cmp2": 12.0,
+               "scat0": 12.5, "voff0": 13.5, "scat1": 15.8, "x0": 13.5, "sig0": 7.0, "sig1": 8.5, "sig2": 11.0, "new": 19.0}}
+CFG.update({'delta': 0.6, 'tol': 0.15, 'step': 17.0, 'due': {'offs0': 1.55, 'offs64': -2.5, 'D0': 2.45, 'D1': 5.25, 'D2': 7.15, 'zq': 1.5, 'yi': 7.25, 'early': 2.0, 'cmp0': 7.45, 'cmp1': 8.9, 'cmp2': 14.5, 'scat0': 11.75, 'voff0': 16.0, 'scat1': 13.3, 'x0': 15.5, 'sig0': 8.75, 'sig1': 7.75, 'sig2': 14.75, 'new': 17.75, 'offs128': 15.5}})
 
-SCRATCH = {
-    "kI": ("sbuf", [128, 2048], "int32"), "Ef": ("sbuf", [128, 2816], "float32"),
-    "X": ("sbuf", [128, 4096], "bfloat16"), "bk3": ("sbuf", [128, 6144], "bfloat16"),
-    "x": ("sbuf", [128, 192], "bfloat16"), "sp": ("sbuf", [128, 12], "int32"), "wt": ("sbuf", [128, 2], "bfloat16"),
-    "ia": ("sbuf", [128, 192], "int32"), "ic": ("sbuf", [128, 192], "int32"), "ic2": ("sbuf", [128, 192], "int32"),
-    "ib": ("sbuf", [128, 128], "int32"), "dgi": ("sbuf", [128, 192], "int32"), "i8": ("sbuf", [128, 8], "int32"),
-    "p0": ("sbuf", [128, 1], "int32"), "p1": ("sbuf", [128, 1], "int32"), "p2": ("sbuf", [128, 1], "int32"),
-    "pm": ("sbuf", [128, 1], "float32"), "pb": ("sbuf", [128, 1], "float32"),
-    "nci": ("sbuf", [128, 768], "int32"), "NC": ("sbuf", [128, 768], "float16"),
-    "dli": ("sbuf", [128, 48], "int32"), "DL": ("sbuf", [128, 48], "float32"), "DLm": ("sbuf", [128, 48], "float32"),
-    "dgS": ("sbuf", [128, 192], "bfloat16"), "LT": ("sbuf", [128, 8, 16], "bfloat16"),
-    "NegI": ("sbuf", [128, 128], "bfloat16"), "NI4": ("sbuf", [128, 128], "bfloat16"),
-    "PI4": ("sbuf", [128, 128], "bfloat16"), "Idb": ("sbuf", [128, 128], "bfloat16"), "xc": ("sbuf", [128, 1024], "bfloat16"),
-    "Idh": ("sbuf", [128, 128], "float16"), "B16": ("sbuf", [128, 128], "bfloat16"),
-    "B16h": ("sbuf", [128, 128], "float16"), "B4h": ("sbuf", [128, 128], "float16"),
-    "BT": ("sbuf", [128, 128], "bfloat16"), "Tri": ("sbuf", [128, 128], "bfloat16"),
-    "tri0": ("sbuf", [128, 128], "bfloat16"), "G8": ("sbuf", [128, 8], "bfloat16"),
-    "Sm": ("sbuf", [128, 2048], "float16"), "RM": ("sbuf", [128, 192], "float32"),
-    "c88": ("sbuf", [128, 192], "float16"),
-    "PW1": ("sbuf", [128, 143], "bfloat16"), "PW2": ("sbuf", [128, 143], "bfloat16"), "P1s": ("sbuf", [128, 143], "bfloat16"),
-    "voff": ("sbuf", [128, 12], "uint16"), "soff": ("sbuf", [128, 12], "uint16"), "vm": ("sbuf", [128, 12], "float32"),
-    "vp1": ("sbuf", [128, 12], "float32"), "vmh": ("sbuf", [128, 12], "float16"), "vmd": ("sbuf", [128, 12], "float32"),
-    "bki": ("sbuf", [128, 12], "int32"), "bka": ("sbuf", [128, 12], "int32"), "bkf": ("sbuf", [128, 12], "float32"),
-    "bmv": ("sbuf", [128, 12], "float32"), "vlw": ("sbuf", [128, 12], "float32"), "ta": ("sbuf", [128, 12], "float32"),
-    "tb": ("sbuf", [128, 12], "float32"), "tc": ("sbuf", [128, 12], "float32"), "ts": ("sbuf", [128, 12], "float32"),
-    "ts2": ("sbuf", [128, 12], "float32"), "vfin": ("sbuf", [128, 12], "float32"),
-    "ev": ("sbuf", [128, 192], "int32"), "Ci": ("sbuf", [128, 192], "int32"), "offs": ("sbuf", [128, 192], "uint16"),
-    "xr": ("sbuf", [128, 2048], "bfloat16"), "diff": ("sbuf", [128, 3072], "bfloat16"),
-    "D": ("sbuf", [128, 3072], "bfloat16"), "sg": ("sbuf", [128, 3072], "bfloat16"), "cmp": ("sbuf", [128, 3072], "bfloat16"),
-    "zd": ("sbuf", [128, 192], "bfloat16"), "z": ("sbuf", [128, 192], "bfloat16"),
-    "hb": ("sbuf", [128, 512], "float32"), "sb": ("sbuf", [128, 512], "float32"), "t2": ("sbuf", [128, 512], "bfloat16"), "u1s": ("sbuf", [128, 256], "float32"),
-    "Pi": ("sbuf", [128, 256], "int32"), "Pd": ("sbuf", [128, 256], "int32"), "He": ("sbuf", [128, 256], "float32"),
-    "h": ("sbuf", [128, 192], "uint16"),
-    "Ki": ("sbuf", [128, 192], "int32"), "emp": ("sbuf", [128, 192], "bfloat16"), "edg": ("sbuf", [128, 192], "bfloat16"),
-    "K2": ("sbuf", [128, 192], "float32"), "Cf": ("sbuf", [128, 192], "float16"), "bigK": ("sbuf", [128, 192], "float32"),
-    "CN": ("sbuf", [128, 384], "bfloat16"), "WW": ("sbuf", [128, 384], "bfloat16"), "isb": ("sbuf", [128, 384], "bfloat16"),
-    "sel": ("sbuf", [128, 384], "bfloat16"), "pay": ("sbuf", [128, 384], "float16"),
-    "wdgw": ("sbuf", [128, 192], "bfloat16"), "gdg": ("sbuf", [128, 192], "float32"), "dn": ("sbuf", [128, 192], "float32"),
-    "sc1": ("sbuf", [128, 192], "float32"), "sc2": ("sbuf", [128, 192], "float32"), "sc3": ("sbuf", [128, 192], "float32"),
-    "cR": ("sbuf", [128, 192], "float32"), "val": ("sbuf", [128, 192], "float32"), "wdg": ("sbuf", [128, 192], "bfloat16"),
-    "q2": ("sbuf", [128, 192], "float32"), "capw": ("sbuf", [128, 192], "bfloat16"), "q3": ("sbuf", [128, 192], "float32"),
-    "EQ": ("sbuf", [128, 12, 192], "bfloat16"), "xy": ("sbuf", [128, 192], "bfloat16"), "xw": ("sbuf", [128, 192], "bfloat16"),
-    "dx": ("sbuf", [128, 192], "bfloat16"),
-    "U0": ("psum", [128, 512], "float32"), "U1": ("psum", [128, 512], "float32"), "O": ("psum", [128, 512], "float32"),
-    "S0": ("psum", [128, 512], "float32"), "S1": ("psum", [128, 512], "float32"), "TB": ("psum", [128, 512], "float32"),
-    "VP": ("psum", [128, 512], "float32"), "CB": ("psum", [128, 512], "float32"),
-}
-SCRATCH["FP"] = ("sbuf", [128, 8 * 144], "bfloat16")
-for _n, _w, _d in (("wf", 2, "bfloat16"), ("zq", 12, "uint16"), ("qi", 12, "uint16"), ("yo", 192, "bfloat16"), ("yi", 192, "bfloat16")):
-    SCRATCH[_n] = ("sbuf", [128, NT * _w], _d)
-PSUM = [n for n in SCRATCH if SCRATCH[n][0] == "psum"]
+f32, bf, h16, i32, u16 = "float32", "bfloat16", "float16", "int32", "uint16"
+SCRATCH = {}
+for _d, _l in (
+    (i32, (("kI", M + PAD), ("sp", 12), ("ia", 192), ("ic", 192), ("ic2", 192), ("ib", 128), ("dgi", 192), ("i8", 8), ("p0", 1), ("p1", 1), ("p2", 1),
+           ("i17", 204), ("j17", 204), ("nci", 768), ("dli", 48), ("ev", 192), ("Ci", 192), ("Pi", 256), ("Pd", 256))),
+    (f32, (("Ef", W + PAD), ("pm", 1), ("pb", 1), ("bk", 1), ("thr", 1), ("dgF", 192), ("H", 192), ("evD", 192), ("dgv", 204), ("sc1", 208), ("sc2", 204),
+           ("sc3", 204), ("b1", 12), ("bmv", 12), ("a1", 192), ("a2", 192), ("u1s", 256), ("He", 256), ("a3", 12), ("winl", 12), ("tc", 12), ("vm", 12), ("vfin", 12))),
+    (bf, (("X", W + PAD), ("bk3", 6144), ("x", 192), ("wt", 2), ("cK", 192), ("cA", 192), ("cR", 192), ("dg17", 204), ("cK17", 204), ("RM", 204),
+          ("c89", 204), ("c12", 128), ("cZ", 68), ("z1", 192), ("xT", 384), ("Rp", 1024), ("Idb", 128), ("NegI", 128), ("N18", 128), ("P18", 128), ("N16", 128), ("P16", 128),
+          ("B16", 128), ("NB18", 128), ("PB18", 128), ("BT", 128), ("NB2k", 128), ("Bo", 128), ("G8", 8), ("Sm", 2048),
+          ("PW1", 143), ("PW2", 143), ("P1s", 143), ("P4s", 143), ("FP", 8 * 144), ("emp", 192), ("sig", 192), ("cap", 192), ("Mc", 192),
+          ("Wc", 192), ("Ws", 192), ("Gm", 192), ("sel", 192), ("EQ", 12 * 204), ("EQd", 204), ("zd", 192), ("z", 192), ("xw", 192), ("Yw", 192),
+          ("t2", 512), ("tb", 12), ("wf", 2 * NT), ("yo", L * NT), ("yi", L * NT))),
+    (h16, (("NC", 768), ("DLh", 48), ("c122", 12), ("vmh", 12), ("Cf", 192), ("CBh", 204), ("pay", 192))),
+    (u16, (("voff", 12), ("soff", 12), ("offs", 192), ("h", 192), ("zq", 12 * NT), ("qi", 12 * NT))),
+):
+    for _n, _w in _l:
+        SCRATCH[_n] = ("sbuf", [128, _w], _d)
+for _n in ("xr", "xc", "diff", "D", "sg", "cmp"):
+    SCRATCH[_n] = ("sbuf", [128, 3072], bf)
+SCRATCH["capD"] = ("sbuf", [128, 204], bf)
+SCRATCH["evD"] = ("sbuf", [128, 12, 17], f32)
+SCRATCH["pay"] = ("sbuf", [128, 12, 17], h16)
+for _n in ("nw", "sel"):
+    SCRATCH[_n] = ("sbuf", [128, 12, 17], bf)
+PSUM = ["DA", "DB", "U0", "U1", "O", "Z", "CB", "TB"]
+for _n in PSUM:
+    SCRATCH[_n] = ("psum", [128, 512] if _n != "Z" else [128, 30, 17], f32)
 NDMA = 16
 SEMAPHORES = ["sV", "sS", "sP", "sG", "lsem", "wa"] + ["qa%d" % t for t in range(NT)] + ["ra%d" % t for t in range(NT)] + ["d%d" % i for i in range(NDMA)]
 
@@ -118,9 +102,10 @@ def tracker(g, T):
             if n in PSUM:
                 bank.setdefault(n, {})[q] = op
 
-    def emit(q, call, reads, writes, dma=False):
+    def emit(q, calls, reads, writes, dma=False):
         waits(q, deps(q, reads, writes, dma))
-        ins = call(eng[q])
+        for call in calls:
+            ins = call(eng[q])
         if dma:
             s, v = "d%d" % used[0], 16
             used[0] += 1
@@ -150,7 +135,7 @@ def tracker(g, T):
 WAKE, SELF = 0.10, 0.10
 
 
-def schedule(plan):
+def schedule(plan, dues):
     n = len(plan)
     pred = [{} for _ in range(n)]
     succ = [{} for _ in range(n)]
@@ -163,6 +148,8 @@ def schedule(plan):
     for i, (q, _c, reads, writes, kind, _d, after) in enumerate(plan):
         for j in after:
             edge(j, i, 0.0)
+            if kind == "d":
+                pred[i][j] = succ[j][i] = -50.0
         for b, lo, hi in reads:
             for x, y, j in wr.get(b, []):
                 if x < hi and lo < y:
@@ -176,15 +163,30 @@ def schedule(plan):
             rd[b] = [e for e in rd.get(b, []) if not (lo <= e[0] and e[1] <= hi)]
         for b, lo, hi in reads:
             rd.setdefault(b, []).append((lo, hi, i))
+    level = [0.0] * n
+    banks = [sorted(set(b for b, _l, _h in p[2] + p[3] if b in PSUM)) for p in plan]
+    for i in range(n - 1, -1, -1):
+        e = min([-level[j] - lat for j, lat in succ[i].items()] + [dues.get(i, NT * CFG["step"] + 3.0)])
+        level[i] = -(e - plan[i][5] - (2.0 if plan[i][4] == "d" else 0.0))
+    best = None
+    for _ in range(CFG["rounds"]):
+        order, end = one_pass(plan, banks, pred, succ, level)
+        if best is None or max(end) < best[0]:
+            best = (max(end), order)
+        _o, level = one_pass(plan, banks, succ, pred, end)
+    return best[1]
+
+
+def one_pass(plan, banks, pred, succ, level):
+    n = len(plan)
     left = [len(p) for p in pred]
     end = [0.0] * n
     early = [0.0] * n
     free, bank, dfree = {}, {}, 0.0
-    banks = [sorted(set(b for b, _l, _h in p[2] + p[3] if b in PSUM)) for p in plan]
     ready = [i for i in range(n) if left[i] == 0]
     order = []
     while ready:
-        best = None
+        at = {}
         for i in ready:
             q = plan[i][0]
             t = max(early[i], free.get(q, 0.0)) if q != "X" else early[i]
@@ -192,10 +194,14 @@ def schedule(plan):
                 for q2, e in bank.get(b, {}).items():
                     if q2 != q and e + WAKE > t:
                         t = e + WAKE
-            key = (round(t / SLOT), i)
-            if best is None or key < best[0]:
-                best = (key, i, t)
-        _k, i, t = best
+            at[i] = t
+        first = min(ready, key=lambda i: (at[i], i))
+        near = [i for i in ready if plan[i][0] == plan[first][0] and at[i] <= at[first] + CFG["delta"]]
+        i = max(near, key=lambda i: (round(level[i], 3), -i))
+        fill = [j for j in near if at[j] + plan[j][5] <= at[i] + CFG["tol"] and at[j] < at[i]]
+        if fill:
+            i = max(fill, key=lambda i: (round(level[i], 3), -i))
+        t = at[i]
         ready.remove(i)
         order.append(i)
         q, kind, d = plan[i][0], plan[i][4], plan[i][5]
@@ -213,10 +219,9 @@ def schedule(plan):
             left[j] -= 1
             if left[j] == 0:
                 ready.append(j)
-    return order
+    return order, end
 
 
-SLOT = 0.02
 ORDER = {}
 
 
@@ -226,102 +231,113 @@ def rank_program(g, core, T, topo):
         return
     emit_now, arrive_now, before, finish = tracker(g, T)
     plan = []
+    TWO = (bf, h16, u16)
+    CYC, PCYC = 0.001, 0.0005
 
     def emit(q, call, reads, writes, dma=False, dur=0.06):
         plan.append((q, [call], reads, writes, "d" if dma else "c", dur, []))
 
-    def cols(x):
-        return x[2] if len(x) > 2 else x[1][0][2] - x[1][0][1]
-
-    def dt_of(x):
-        return SCRATCH.get(x[1][0][0], ("sbuf", 0, "bfloat16"))[2]
-
-    def in_psum(x):
-        return x[1][0][0] in PSUM
-
-    CYC = 0.00085
-
-    def time_of(out, a, b=None):
-        if len(a) > 3:
-            return 0.06 + 1.56 * CYC * cols(out)
-        if len(out) > 3:
-            return 0.06 + 3.8 * CYC * cols(a)
-        n = cols(out)
-        if b is not None:
-            f = 1.0 if in_psum(a) or in_psum(b) else 2.0
-        else:
-            f = 0.5 if not in_psum(a) and not in_psum(out) and dt_of(a) in TWO and dt_of(out) in TWO else 1.0
-        return CYC * max(64, f * n)
-    TWO = ("bfloat16", "float16", "uint16")
-    group = []
-    width = {n: (SCRATCH[n][1][1] if len(SCRATCH[n][1]) == 2 else SCRATCH[n][1][1] * SCRATCH[n][1][2]) for n in SCRATCH}
-
     def o(n, lo=0, hi=None, step=1):
-        hi = width[n] if hi is None else hi
-        return (T[n][:, lo:hi] if step == 1 else T[n][:, lo:hi:step], [(n, lo, hi)], (hi - lo + step - 1) // step)
+        hi = SCRATCH[n][1][1] if hi is None else hi
+        return (T[n][:, lo:hi] if step == 1 else T[n][:, lo:hi:step], [(n, lo, hi)], (hi - lo + step - 1) // step, n, False)
+
+    def o3(n, lo, hi, k=None):
+        ap = T[n][:, 16 * lo:16 * hi] if k is None else T[n][:, 16 * lo + k:16 * hi:16]
+        names = [n] if n != "xr" else ["xr%d" % j for j in (range(16) if k is None else [k])]
+        return (ap, [(m, lo, hi) for m in names], (hi - lo) * (16 if k is None else 1), n, False)
+
+    def o17(n, c0, c1, k0):
+        return (T[n][:, c0:c1, k0:17], [(n, 17 * c0, 17 * c1)], (c1 - c0) * (17 - k0), n, False)
 
     def ind(n, lo, hi, off):
-        return (T[n][:, lo:hi].indirect(off[0]), [(n, lo, hi)] + off[1], 16 * off[2], "indirect")
+        return (T[n][:, lo:hi].indirect(off[0]), [(n, lo, hi)] + off[1], 16 * off[2], n, True)
 
     def sca(s):
         return (s[0], s[1]) if isinstance(s, tuple) else (s, [])
 
+    def time_of(out, a, b=None):
+        if a[4]:
+            return 0.06 + 1.56 * CYC * out[2]
+        if out[4]:
+            return 0.06 + 3.8 * CYC * out[2]
+        if b is not None:
+            f = 1.0 if a[3] in PSUM or b[3] in PSUM else 2.0
+        else:
+            f = 0.5 if SCRATCH[a[3]][2] in TWO and SCRATCH[out[3]][2] in TWO else 1.0
+        return CYC * max(64, f * out[2])
+
     def tt(out, a, b, op):
-        emit("V", lambda e: e.tensor_tensor(out[0], a[0], b[0], op), a[1] + b[1], out[1], dur=time_of(out, a, b))
+        rd_, wr_ = (out[1][1:], out[1][:1]) if out[4] else ([], out[1])
+        emit("V", lambda e: e.tensor_tensor(out[0], a[0], b[0], op), a[1] + b[1] + rd_, wr_, dur=time_of(out, a, b))
 
     def ts(out, a, s1, op0, s2=None, op1=None):
-        s1 = sca(s1)
+        s1, s2 = sca(s1), sca(s2)
         if op1 is None:
             emit("V", lambda e: e.tensor_scalar(out[0], a[0], s1[0], None, op0), a[1] + s1[1], out[1], dur=time_of(out, a))
         else:
-            emit("V", lambda e: e.tensor_scalar(out[0], a[0], s1[0], s2, op0, op1), a[1] + s1[1], out[1], dur=time_of(out, a))
+            emit("V", lambda e: e.tensor_scalar(out[0], a[0], s1[0], s2[0], op0, op1), a[1] + s1[1] + s2[1], out[1], dur=time_of(out, a))
 
     def cp(out, a):
-        emit("V", lambda e: e.tensor_copy(out[0], a[0]), a[1] + out[1][1:], out[1][:1], dur=time_of(out, a))
+        emit("V", lambda e: e.tensor_copy(out[0], a[0]), a[1], out[1], dur=time_of(out, a))
 
     def ms(out, c):
-        emit("V", lambda e: e.memset(out[0], c), [], out[1], dur=CYC * cols(out))
+        emit("V", lambda e: e.memset(out[0], c), [], out[1], dur=time_of(out, out))
 
-    def scan(out, a, b):
-        emit("V", lambda e: e.tensor_tensor_scan(out[0], a[0], b[0], 0.0, A.mult, A.add), a[1] + b[1], out[1], dur=CYC * cols(out))
+    def scan(out, a, b, op0, op1):
+        emit("V", lambda e: e.tensor_tensor_scan(out[0], a[0], b[0], 0.0, op0, op1), a[1] + b[1], out[1], dur=CYC * max(64, out[2]))
 
     def act(out, a, func, scale=1.0, bias=0.0):
-        emit("S", lambda e: e.activation(out[0], a[0], func, bias=bias, scale=scale), a[1], out[1],
-             dur=0.065 + CYC * cols(a) * (1.56 if len(a) > 3 else 1.0))
+        s, b = sca(scale), sca(bias)
+        emit("S", lambda e: e.activation(out[0], a[0], func, bias=b[0], scale=s[0]), a[1] + s[1] + b[1], out[1],
+             dur=0.065 + CYC * out[2] * 1.56 if a[4] else CYC * max(64, out[2]))
 
-    def mm(out, lhsT, rhs, start, stop, whole=None, cut=False):
-        group.append((lambda e: e.matmul(out[0], lhsT[0], rhs[0], start, stop), lhsT[1] + rhs[1], out[1] + ([(whole, 0, 512)] if whole else []),
-                      0.0007 * max(64, cols(rhs)) * (4 if dt_of(rhs) == "float32" else 1)))
-        if stop or cut:
-            plan.append(("P", [c[0] for c in group], sorted(set(x for c in group for x in c[1])), sorted(set(x for c in group for x in c[2])),
-                         "c", sum(c[3] for c in group), []))
-            del group[:]
+    def mm(terms, add=False, more=False):
+        calls, rd_, wr_, dur = [], [], [], 0.0
+        for i, (out, lhsT, rhs) in enumerate(terms):
+            calls.append(lambda e, out=out, lhsT=lhsT, rhs=rhs, i=i: e.matmul(out[0], lhsT[0], rhs[0], i == 0 and not add, i == len(terms) - 1 and not more))
+            rd_ += lhsT[1] + rhs[1]
+            wr_ += out[1]
+            dur += PCYC * max(64, rhs[2])
+        mark = [(terms[0][0][3] + "start", 0, 1)]
+        if add and more:
+            rd_ += mark + wr_
+        elif add:
+            rd_ += wr_
+            wr_ += mark
+        else:
+            wr_ += mark
+        plan.append(("P", calls, sorted(set(rd_)), sorted(set(wr_)), "c", dur, []))
 
     def iota(n, pattern, base, cm):
         b = o(n)
-        emit("G", lambda e: e.iota(b[0], pattern, base, cm), [], b[1], dur=0.15 + 2 * CYC * cols(b))
+        emit("G", lambda e: e.iota(b[0], pattern, base, cm), [], b[1], dur=0.15 + 2 * CYC * b[2])
 
     def load(q, name, lo, hi, src):
         b = o(name, lo, hi)
-        emit(q, lambda e: e.dma_start(b[0], src), [], b[1], dma=True, dur=0.0013 * cols(b) * (1 if dt_of(b) in TWO else 2))
+        emit(q, lambda e: e.dma_start(b[0], src), [], b[1], dma=True, dur=0.0013 * b[2] * (1 if SCRATCH[name][2] in TWO else 2))
 
     def store(q, dst, b):
-        emit(q, lambda e: e.dma_start(dst, b[0]), b[1], [], dma=True, dur=0.0013 * cols(b) * (1 if dt_of(b) in TWO else 2))
+        emit(q, lambda e: e.dma_start(dst, b[0]), b[1], [], dma=True, dur=0.0013 * b[2] * (1 if SCRATCH[b[3]][2] in TWO else 2))
 
     load("S", "wt", 0, 2, T.wts[:, :])
     load("Y", "sp", 0, 12, T.spot[:, :])
-    load("Y", "kI", 0, 2048, T.kids[:, :])
+    load("Y", "kI", PAD, M + PAD, T.kids[:, :])
     load("S", "x", 0, 192, T.cand[:, :])
-    load("Y", "X", 0, 2048, T.nodes[:, :])
+    load("Y", "X", PAD, M + PAD, T.nodes[:, :])
     for j in range(3):
         load("Y", "bk3", 2048 * j, 2048 * j + 2048, T.book[:, :])
+    loads = [i for i in range(len(plan)) if plan[i][0] == "Y"]
+    for a_, b_ in zip(loads, loads[1:]):
+        plan[a_][3].append(("ld%d" % b_, 0, 0))
+        plan[b_][6].append(a_)
 
     iota("p0", [[0, 1]], 0, 1)
     iota("ia", [[1, 192]], 1024, -1)
     iota("ic", [[1, 192]], 0, 0)
     iota("i8", [[1, 8]], 0, 0)
-    iota("dli", [[16, 48]], 2048, 0)
-    iota("nci", [[1, 768]], -2047, 0)
+    iota("i17", [[0, 12], [1, 17]], 1023, -1)
+    iota("dli", [[16, 48]], M + PAD - 1424, 0)
+    iota("nci", [[1, 768]], 0, 0)
 
     allto = [T.cores[(r - 1 - t) % N] for t in range(NT)]
     common = [e for e in topo.engines(core, allto[0]) if all(e in topo.engines(core, c) for c in allto)][:8]
@@ -351,342 +367,294 @@ def rank_program(g, core, T, topo):
         sends.append(len(plan))
         plan.append(("G", [call], [(in_n, lo, hi)], [], "s", 1.0, []))
 
-    ms(o("X", 2048, 4080), 0.0)
-    ms(o("X", 4080, 4096), 512.0)
-    ms(o("Ef", 2048, 2816), 4095.0)
-    for n in ("PW1", "PW2", "P1s", "FP"):
+    ms(o("X", 0, PAD), 512.0)
+    ms(o("kI", 0, PAD), 0)
+    ms(o("Ef", 0, PAD), 0.0)
+    for n in ("PW1", "PW2", "P1s", "P4s"):
         ms(o(n), 0.0)
-    cp(o("voff"), o("sp"))
-    ts(o("vm"), o("sp"), -1408.0, A.add)
-    ts(o("vp1"), o("sp"), 1.0, A.add)
-    cp(o("vmh"), o("vm"))
+    for t in range(NT):
+        ms(o("FP", 288 * t, 288 * t + 288), 0.0)
+    for n, c in (("c89", 89.0), ("c12", C12), ("cZ", -65536.0)):
+        ms(o(n), c)
+    ms(o("sc1", 0, 4), 0.0)
+    ms(o17("evD", 0, 12, 0), BIG)
+    ts(o("voff"), o("sp"), float(PAD), A.add)
+    ts(o("vmh"), o("sp"), -1408.0, A.add)
     ts(o("p1"), o("p0"), 15, A.bitwise_and)
     cp(o("pm"), o("p1"))
     ts(o("p2"), o("p0"), 4, A.arith_shift_right)
     cp(o("pb"), o("p2"))
+    ts(o("c122"), o("c89", 0, 12), 0.0, A.mult, (C10 - 1408.0) / 16, A.add)
     ts(o("dgi"), o("ia"), 15, A.bitwise_and)
-    ts(o("dgS"), o("dgi"), 0.0, A.is_equal)
-    dgP = lambda lo, hi: o("VP", lo, hi)
-    ts(o("VP", 0, 192), o("dgi"), 0.0, A.is_equal)
-    ts(o("NegI"), o("ia", 0, 128), 1024.0, A.is_equal, -1.0, A.mult)
-    ts(o("NI4"), o("ia", 0, 128), 1024.0, A.is_equal, -1.0 / 4096, A.mult)
-    ts(o("PI4"), o("ia", 0, 128), 1024.0, A.is_equal, 1.0 / 4096, A.mult)
+    ts(o("dgF"), o("dgi"), 0.0, A.is_equal)
+    act(o("cK"), o("dgF"), F.Identity, scale=BIG, bias=-BIG)
+    act(o("cA"), o("dgF"), F.Identity, scale=PAD - BIG, bias=-float(PAD))
+    act(o("cR"), o("dgF"), F.Identity, scale=-4096.0, bias=M + 32768.0 + 4096.0 - BIG)
+    act(o("H"), o("dgF"), F.Identity, scale=BIG - 4095.0, bias=4095.0)
     ts(o("Idb"), o("ia", 0, 128), 1024.0, A.is_equal)
-    ts(o("Idh"), o("ia", 0, 128), 1024.0, A.is_equal)
     ts(o("ib"), o("ic", 0, 128), 4, A.arith_shift_right)
     ts(o("B16"), o("ib"), o("pb"), A.is_equal)
-    cp(o("B16h"), o("B16"))
-    ts(o("B4h"), o("B16"), 4096.0, A.mult)
-    ts(o("BT"), o("B16"), 3.0 / 64, A.mult)
-    ts(o("tri0"), o("ia", 0, 128), 1024.0, A.is_gt)
-    tt(o("Tri"), o("tri0"), o("B16"), A.mult)
+    for n, c in (("NegI", -1.0), ("N18", -BIG), ("P18", BIG), ("N16", -65536.0), ("P16", 65536.0)):
+        act(o(n), o("Idb"), F.Copy, scale=c)
+    for n, c in (("NB18", -BIG), ("PB18", BIG), ("BT", 0.4), ("NB2k", -2048.0), ("Bo", 1424.0)):
+        act(o(n), o("B16"), F.Copy, scale=c)
     ts(o("G8"), o("i8"), o("pb"), A.is_equal)
     ts(o("P1s", 15, 143, 16), o("G8"), 1.0, A.mult)
-    ts(o("ic2"), o("ic"), 15, A.bitwise_and)
-    ts(o("RM"), o("ic2"), 0.0, A.is_gt)
-    for e_ in range(8):
-        ts((T.LT[:, e_, :], [("LT", 16 * e_, 16 * e_ + 16)]), o("ic", 0, 16), o("pm"), A.is_gt)
-    ts(o("c88"), o("RM"), 0.0, A.mult, 88.0625, A.add)
-    for m in range(16):
-        ts(o("Sm", 128 * m, 128 * m + 128), o("B16h"), o("dgS", m, m + 1), A.mult)
-    ts(o("DL"), o("dli"), o("pm"), A.add)
-    ts(o("DLm"), o("DL"), -1408.0, A.add)
-    cp(o("NC"), o("nci"))
+    ts(o("P4s", 15, 143, 16), o("G8"), 4096.0, A.mult)
     ts(o("PW1", 15, 143, 16), o("G8"), o("wt", 0, 1), A.mult)
     ts(o("PW2", 15, 143, 16), o("G8"), o("wt", 1, 2), A.mult)
+    ms(o("RM"), 1.0)
+    ms(o("RM", 0, 204, 17), 0.0)
+    ms(o17("sel", 0, 12, 0), 0.0)
+    ms(o17("pay", 0, 12, 0), 0.0)
+    for m in range(16):
+        act(o("Sm", 128 * m, 128 * m + 128), o("B16"), F.Copy, scale=o("dgF", m, m + 1))
+    ts(o("j17"), o("i17"), 15, A.bitwise_and)
+    ts(o("dg17"), o("j17"), 0.0, A.is_equal)
+    act(o("cK17"), o("dg17"), F.Identity, scale=-BIG, bias=2 * BIG)
+    ms(o("cK17", 0, 204, 17), 2 * BIG)
+    ms(o("dg17", 0, 204, 17), 1.0)
+    ts(o("DLh"), o("dli"), o("pm"), A.add)
+    cp(o("NC"), o("nci"))
+    SA = 16 * LNB / 4096
+    act(o("bk"), o("pm"), F.Identity, scale=-LNB, bias=15 * LNB - 79.3 + 65536.0 * SA)
+    act(o("thr"), o("pm"), F.Exp, scale=LN32, bias=math.log(24.0))
+
+    dues = {}
+
+    def due(t, name):
+        if name in CFG["due"]:
+            dues[len(plan) - 1] = t * CFG["step"] + CFG["due"][name]
 
     def window(n, k, base=0):
         return o(n, base + 15 - k, base + 143 - k)
 
-    def repeat():
+    def repeat(lo, hi):
         for k in range(16):
-            act((T.xr[:, k:2048:16], [("xr%d" % k, 0, 2048)]), o("x", 0, 128), F.Copy)
-
-    repeat()
+            if CFG["xr"] == "S":
+                act(o3("xr", lo, hi, k), o("x", lo, hi), F.Copy)
+            else:
+                cp(o3("xr", lo, hi, k), o("x", lo, hi))
 
     CH = ((0, 64), (64, 128), (128, 192))
     UB = ("U0", "U1", "U0")
-    deferred = []
 
-    def gather_slots(t, lo, hi):
-        tab = ("kI", 0, 2048) if t == 0 else ("Ef", 0, W)
-        cp(o("ev", lo, hi), ind(tab[0], tab[1], tab[2], o("voff", lo // 16, hi // 16)))
-        ts(o("Ci", lo, hi), o("ev", lo, hi), 4095, A.bitwise_and)
-        cp(o("offs", lo, hi), o("Ci", lo, hi))
+    def half(n, lo, hi, step=1):
+        x_ = o(n, lo, hi, step)
+        return (T[n][0:64, lo:hi] if step == 1 else T[n][0:64, lo:hi:step],) + x_[1:]
 
-    def hash_mod(U, n, w):
-        c = (128 * w, 128 * w + 2 * n)
-        act(o("sb", *c), o(U, 0, 2 * n), F.Identity, bias=-2047.5)
-        act(o("hb", *c), o("sb", *c), F.Identity, bias=BIGM)
-        act(o("t2", *c), o("hb", *c), F.Identity, bias=-BIGM)
+    def turn(c, bank, at, less):
+        p = half(bank, at, at + 128)
+        mm([(p, o("x", *CH[c]), o("Idb"))] + ([(p, o("Yw", *CH[c]), o("NegI"))] if less else []))
+        act(half("xT", 128 * c, 128 * c + 128), p, F.Abs)
 
-    def hash_end(U, n, w, out):
+    for k in range(16):
+        act(half("Rp", k, 1024, 16), half("NegI", 0, 64), F.Copy)
+    for c in range(3):
+        if CFG["path"][c] == "V":
+            repeat(*CH[c])
+        else:
+            turn(c, "TB", 128 * c, False)
+
+    def hash_(U, n, w, out, once):
         c = (64 * w, 64 * w + n)
         u2 = o(U, n, 2 * n)
-        tt(u2, u2, o("t2", 128 * w + n, 128 * w + 2 * n), A.subtract)
+        act(o("t2", 128 * w, 128 * w + 2 * n), o(U, 0, 2 * n), F.Identity, bias=-2047.5)
         tt(o("u1s", *c), o(U, 0, n), o("t2", 128 * w, 128 * w + n), A.subtract)
+        tt(u2, u2, o("t2", 128 * w + n, 128 * w + 2 * n), A.subtract)
         tt(o("Pi", *c), o("u1s", *c), u2, A.mult)
         ts(o("Pd", *c), o("Pi", *c), 5, A.arith_shift_right, 2047, A.bitwise_and)
-        tt(o("He", *c), o("Pd", *c), u2, A.add)
-        cp(out, o("He", *c))
+        if once:
+            tt(o("Pi", *c), o("Pd", *c), u2, A.add)
+            ts(o("Pd", *c), o("Pi", *c), 2047, A.bitwise_and)
+            cp(out, o("Pd", *c))
+        else:
+            tt(o("He", *c), o("Pd", *c), u2, A.add)
+            cp(out, o("He", *c))
 
     for t in range(NT):
         last = t == NT - 1
         b = T.cores[(r + 1 + t) % N]
         asker = T.cores[(r - 1 - t) % N]
+        nl = PAD + M + L * t
+        books = 2048 if t == 0 else 6144
+        stood = PAD + M + L * max(t - 1, 0)
 
-        def XG(c):
-            lo, hi = CH[c]
-            dv = o("diff", 16 * lo, 16 * hi)
-            xg = ind("X", 0, 4096, o("offs", lo, hi))
-            xv = (T.xr[:, 16 * lo:16 * hi], [("xr%d" % k, 16 * lo, 16 * hi) for k in range(16)])
-            tt(dv, xg, xv, A.subtract)
-            act(o("D", 16 * lo, 16 * hi), dv, F.Abs)
-
-        def usum(c, j):
-            lo, hi = CH[c]
-            U = UB[c]
-            for k in range(16):
-                mm(o(U, 64 * j, 64 * j + 64), window("PW%d" % (j + 1), k), o("D", 16 * lo + k, 16 * hi, 16), k == 0, k == 15)
-
-        def BG(c):
-            lo, hi = CH[c]
-            tt(o("cmp", 16 * lo, 16 * hi), ind("bk3", 0, 6144, o("h", lo, hi)), o("D", 16 * lo, 16 * hi), A.is_ge)
-
-        def sign(c):
-            lo, hi = CH[c]
-            if c == 2:
-                for hf in range(2):
-                    act(o("sg", 2048 + 512 * hf, 2560 + 512 * hf), o(("TB", "S1")[hf]), F.Sign, scale=-1.0, bias=0.5)
-            else:
-                ts(o("sg", 16 * lo, 16 * hi), o("diff", 16 * lo, 16 * hi), 0.0, A.is_le)
-
-        def over(c):
-            lo, hi = CH[c]
-            for k in range(16):
-                mm(o("O", lo, hi), window("P1s", k), o("sg", 16 * lo + k, 16 * hi, 16), k == 0, k == 15)
-
-        def ssum(c):
-            lo, hi = CH[c]
-            so = o("S0", lo, hi) if c < 2 else o("S1", 0, 64)
-            mm(so, o("PI4"), o("emp", lo, hi), True, False)
-            mm(so, o("NI4"), o("edg", lo, hi), False, False)
-            for k in range(16):
-                mm(so, window("P1s", k), o("cmp", 16 * lo + k, 16 * hi, 16), False, k == 15)
-
-        gather_slots(t, 0, 64)
+        for lo, hi in CFG["ev"]:
+            ts(o("ev", lo, hi), ind("kI" if t == 0 else "Ef", 0, stood, o("voff", lo // 16, hi // 16)), float(PAD), A.add)
+            ts(o("Ci", lo, hi), o("ev", lo, hi), 4095, A.bitwise_and)
+            cp(o("offs", lo, hi), o("Ci", lo, hi))
+            due(t, "offs%d" % lo)
         if t == 0:
-            gather_slots(t, 64, 192)
-            cp(o("Ef", 0, 2048), o("kI"))
-            for j in range(2 * NT):
-                ts(o("FP", 144 * j + 15, 144 * j + 143, 16), o("G8"), o("wf", j, j + 1), A.mult)
-        tt(o("zd"), ind("X", 0, 4096, o("voff")), o("x"), A.subtract)
-        act(o("z"), o("zd"), F.Abs)
-        if t > 0:
-            gather_slots(t, 64, 192)
-        act(o("xc"), ind("X", 0, 4096, o("offs", 128, 192)), F.Copy)
-        for j in range(2):
-            for m in range(16):
-                mm(o("U1", 12 * j, 12 * j + 12), window("FP", m, 144 * (2 * t + j)), o("z", m, 192, 16), m == 0, m == 15)
-        XG(0)
-        for f in deferred:
-            f()
-        del deferred[:]
-        usum(0, 0)
-        hash_mod("U1", 12, 3)
-        usum(0, 1)
-        XG(1)
-        ts(o("emp"), o("Ci"), 4095.0, A.is_equal, -4096.0, A.mult)
-        ts(o("Ki"), o("ev"), 12, A.arith_shift_right)
-        hash_end("U1", 12, 3, o("zq", 12 * t, 12 * t + 12))
-        send(b, "qi", "zq", 12 * t, 12 * t + 12, "qa%d" % t)
-        arrive("qa%d" % t, len(topo.engines(asker, core)[:8]), "qi", 12 * t, 12 * t + 12, 3.5)
-        for hf in range(2):
-            bank = ("TB", "S1")[hf]
-            mm(o(bank), o("Idb"), o("xc", 512 * hf, 512 * hf + 512), True, False)
-            for k in range(16):
-                mm(o(bank, k, 512, 16), o("NegI"), o("x", 128 + 32 * hf, 160 + 32 * hf), False, k == 15)
-        hash_mod("U0", 64, 0)
-        for hf in range(2):
-            act(o("D", 2048 + 512 * hf, 2560 + 512 * hf), o(("TB", "S1")[hf]), F.Abs)
-        usum(1, 0)
-        usum(1, 1)
-        sign(0)
-        tt(o("edg"), dgP(0, 192), o("emp"), A.mult)
-        ts(o("Cf"), o("Ci"), -1408.0, A.add)
-        tt(o("K2"), o("Ki"), o("edg"), A.add)
-        hash_end("U0", 64, 0, o("h", 0, 64))
-        BG(0)
-        hash_mod("U1", 64, 1)
-        usum(2, 0)
-        usum(2, 1)
-        sign(2)
-        ts(o("VP", 256, 448), o("ev"), -1.0, A.mult, 4095.0, A.add)
-        hash_end("U1", 64, 1, o("h", 64, 128))
-        BG(1)
-        mm(o("CB", 0, 192), o("B16h"), o("c88"), True, False)
-        for m in range(16):
-            mm(o("CB", m, 192, 16), o("Sm", 128 * m, 128 * m + 128), o("vmh"), False, m == 15)
-        over(0)
-        hash_mod("U0", 64, 2)
-        ssum(0)
-        sign(1)
-        over(1)
-        act(o("yo", L * t, L * t + L), ind("bk3", 0, 6144, o("qi", 12 * t, 12 * t + 12)), F.Copy)
-        send(asker, "yi", "yo", L * t, L * t + L, "ra%d" % t)
-        arrive("ra%d" % t, len(topo.engines(b, core)[:8]), "yi", L * t, L * t + L, 4.5)
-        act(o("O", 192, 320), o("O", 0, 128), F.Relu, scale=-128.0, bias=1216.0)
-        hash_end("U0", 64, 2, o("h", 128, 192))
-        BG(2)
-        ssum(1)
-        tt(o("vmd"), o("vm"), o("DLm", 12 * t, 12 * t + 12), A.subtract)
+            for j in range(4):
+                cp(o("Ef", PAD + 512 * j, PAD + 512 * j + 512), o("kI", PAD + 512 * j, PAD + 512 * j + 512))
+        for j in range(2 * t, 2 * t + 2):
+            ts(o("FP", 144 * j + 15, 144 * j + 143, 16), o("G8"), o("wf", j, j + 1), A.mult)
 
-        def batch(lo, hi, SB, t=t, last=last):
+        tt(o("zd"), ind("X", 0, stood, o("voff")), o("x"), A.subtract)
+        act(o("z"), o("zd"), F.Abs)
+        mm([(o("U1", 0, 24), o("Idb"), o("c12", 0, 24))] +
+           [(o("U1", 12 * j, 12 * j + 12), window("FP", m, 144 * (2 * t + j)), o("z", m, 192, 16)) for j in range(2) for m in range(16)])
+        hash_("U1", 12, 3, o("zq", 12 * t, 12 * t + 12), t == 0)
+        due(t, "zq")
+        send(b, "qi", "zq", 12 * t, 12 * t + 12, "qa%d" % t)
+        arrive("qa%d" % t, len(topo.engines(asker, core)[:8]), "qi", 12 * t, 12 * t + 12, 2.0)
+        act(o("yo", L * t, L * t + L), ind("bk3", 0, books, o("qi", 12 * t, 12 * t + 12)), F.Copy)
+        due(t, "yi")
+        send(asker, "yi", "yo", L * t, L * t + L, "ra%d" % t)
+        arrive("ra%d" % t, len(topo.engines(b, core)[:8]), "yi", L * t, L * t + L, 3.0)
+
+        ts(o("emp"), o("offs"), float(PAD - 1), A.is_equal)
+        ts(o("Cf"), o("offs"), -1424.0, A.add)
+        mm([(o("O", 192, 384), o("Idb"), o("cK")), (o("O", 192, 384), o("N18"), o("emp"))])
+        tt(o17("evD", 0, 12, 1), o("O", 192, 384), o("ev"), A.add)
+        due(t, "early")
+        mm([(o17("Z", 12, 24, 1), o("Idb"), o("Cf"))])
+        mm([(o("CB", 0, 204), o("B16"), o("c89"))] +
+           [(o("CB", 1 + m, 204, 17), o("Sm", 128 * m, 128 * m + 128), o("vmh")) for m in range(16)] +
+           [(o("CB", 0, 204, 17), o("Idb"), o("DLh", 12 * t, 12 * t + 12))])
+        ts(o("CBh", 17, 204), o("CB", 17, 204), -1424.0, A.add)
+        due(t, "early")
+        tt(o("dgv"), o("CB", 0, 204), o("dg17"), A.mult)
+        due(t, "early")
+
+        for c, (lo, hi) in enumerate(CH):
+            U = UB[c]
+            zero_one = CFG["sign"][c] == "V"
+            if CFG["path"][c] == "V":
+                w = (hi - lo) // CFG["piece"]
+                for a in range(lo, hi, w):
+                    tt(o3("diff", a, a + w), ind("X", 0, nl, o("offs", a, a + w)), o3("xr", a, a + w), A.subtract)
+                    act(o3("D", a, a + w), o3("diff", a, a + w), F.Abs)
+                    due(t, "D%d" % c)
+                if zero_one:
+                    ts(o3("sg", lo, hi), o3("diff", lo, hi), 0.0, A.is_le)
+                else:
+                    act(o3("sg", lo, hi), o3("diff", lo, hi), F.Sign, scale=-1.0, bias=0.5)
+            else:
+                for hf, bank in enumerate(("DA", "DB")):
+                    a, e = lo + 32 * hf, lo + 32 * hf + 32
+                    act(o3("xc", a, e), ind("X", 0, nl, o("offs", a, e)), F.Copy)
+                    mm([(o(bank), half("xT", 128 * c, 128 * c + 128), half("Rp", 512 * hf, 512 * hf + 512)), (o(bank), o("Idb"), o3("xc", a, e))])
+                    act(o3("D", a, e), o(bank), F.Abs)
+                    due(t, "D%d" % c)
+                    if zero_one:
+                        ts(o3("sg", a, e), o(bank), 0.0, A.is_le)
+                    else:
+                        act(o3("sg", a, e), o(bank), F.Sign, scale=-1.0, bias=0.5)
+            mm([(o(U, 0, 128), o("Idb"), o("c12"))] +
+               [(o(U, 64 * j, 64 * j + 64), window("PW%d" % (j + 1), k), o3("D", lo, hi, k)) for j in range(2) for k in range(16)])
+            hash_(U, 64, c, o("h", lo, hi), t == 0)
+            w = (hi - lo) // CFG["bg"]
+            for a in range(lo, hi, w):
+                tt(o3("cmp", a, a + w), ind("bk3", 0, books, o("h", a, a + w)), o3("D", a, a + w), A.is_ge)
+                due(t, "cmp%d" % c)
+            mm([(o("O", lo, hi), window("P1s", k), o3("sg", lo, hi, k)) for k in range(16)])
+            act(o("sig", lo, hi), o("O", lo, hi), F.Sign, scale=-1.0, bias=9.5 if zero_one else 3.0)
+            due(t, "sig%d" % c)
+            Z = o17("Z", lo // 16, hi // 16, 1)
+            mm([(o17("Z", lo // 16, hi // 16, 0), o("Idb"), o("cZ")), (Z, o("N16"), o("sig", lo, hi))] +
+               [(Z, window("P4s", k), o3("cmp", lo, hi, k)) for k in range(16)])
+
+        yi = lambda lo, hi: o("yi", L * t + lo, L * t + hi)
+        mm([(o("O", 192, 384), o("Idb"), o("x")), (o("O", 192, 384), o("NegI"), yi(0, L))])
+        act(o("xw"), o("O", 192, 384), F.Abs)
+        mm([(o("U1", 0, 12), o("B16"), o("c122"))] + [(o("U1", 0, 12), window("PW1", m), o("xw", m, 192, 16)) for m in range(16)])
+        act(o("tb"), o("U1", 0, 12), F.Identity, bias=1408.0 - 511.5)
+        tt(o("b1"), o("U1", 0, 12), o("tb"), A.subtract)
+        tt(o("bmv"), o("b1"), o("vmh"), A.subtract)
+
+        for bi, (lo, hi, TB, to, XB, xo) in enumerate(((0, 128, "TB", (0, 128, 256, 384, 384, 0), "DB", (0, 128, 256, 384)),
+                                                       (128, 192, "DA", (0, 64, 128, 192, 256, 320), "O", (0, 64, 128, 384)))):
             n = hi - lo
             c0, c1 = lo // 16, hi // 16
-            a, e = 2 * lo, 2 * lo + n
-            z_ = 2 * hi
-            T0, L0, W0 = (0, 256, 256) if lo == 0 else (384, 384, 0)
-            S = o(SB, 0, n)
-            EX = o(SB, n, 2 * n)
-            Q1 = o(SB, 2 * n, 3 * n)
-            last_lane = lambda nm: o(nm, lo + 15, hi, 16)
+            e0, e1 = 17 * c0, 17 * c1
+            s = lambda nm: o(nm, lo, hi)
             lst = lambda nm: o(nm, c0, c1)
-
-            def d1():
-                act(EX, S, F.Exp, scale=LN32)
-                act(Q1, S, F.Identity, scale=4096.0, bias=-4095.0)
-                tt(o("bigK", lo, hi), o("O", 192 + lo, 192 + hi), o("K2", lo, hi), A.add)
-                tt(o("CN", e, z_), S, o("bigK", lo, hi), A.is_gt)
-                tt(o("CN", a, e), S, o("bigK", lo, hi), A.is_le)
-                tt(o("WW", a, e), EX, o("CN", a, e), A.mult)
-                tt(o("WW", e, z_), EX, o("CN", e, z_), A.mult)
-                mm(o("TB", T0, T0 + 2 * n), o("BT"), o("WW", a, z_), True, True)
-
-            def d2():
-                tt(o("wdgw", lo, hi), dgP(lo, hi), o("CN", e, z_), A.mult)
-                scan(o("sc1", lo, hi), o("RM", lo, hi), o("wdgw", lo, hi))
-                tt(o("isb", a, z_), o("WW", a, z_), o("TB", T0, T0 + 2 * n), A.is_gt)
-                mm(o("TB", L0, L0 + 2 * n), o("Tri"), o("isb", a, z_), True, True)
-
-            def d3():
-                tt(lst("vlw"), last_lane("sc1"), lst("vp1"), A.mult)
-                tt(o("gdg", lo, hi), dgP(lo, hi), o("CN", a, e), A.mult)
-                tt(Q1, Q1, o("Ci", lo, hi), A.add)
-                tt(o("sel", a, z_), o("isb", a, z_), o("TB", L0, L0 + 2 * n), A.is_gt)
-                tt(o("pay", e, z_), S, o("sel", e, z_), A.mult)
-                tt(o("pay", a, e), o("sel", a, e), o("Cf", lo, hi), A.mult)
-                mm(o("TB", T0 + n, T0 + 2 * n), o("Idh"), o("NC", L * t + lo, L * t + hi), True, False)
-                mm(o("TB", T0 + n, T0 + 2 * n), o("B4h"), o("pay", e, z_), False, True)
-                mm(o("TB", T0, T0 + n), o("B16h"), o("pay", a, e), True, True)
-
-            def d4():
-                for c in range(c0, c1):
-                    ts((T.EQ[:, c, 0:L - 16 * c], [("EQ", L * c, L * c + L - 16 * c)]), o("CB", 16 * c, L), o("vlw", c, c + 1), A.is_equal)
-                eqd = (T.EQ[:, c0:c1, 0:16], [("EQ", L * c0, L * c1)], 16 * (c1 - c0))
-                tt(eqd, eqd, (T.LT[:, 0:c1 - c0, :], [("LT", 0, 16 * (c1 - c0))]), A.mult)
-
-                def count(cs, x0, x1, first, final):
-                    for c in cs:
-                        s = max(x0, 16 * c)
-                        mm(o("CB", 192 + s, 192 + x1), o("B16"), (T.EQ[:, c, s - 16 * c:x1 - 16 * c], [("EQ", L * c, L * c + L)], x1 - s),
-                           first and c == cs[0], final and c == cs[-1])
-                if lo == 0:
-                    count(list(range(8)), 0, 128, True, True)
-                else:
-                    count(list(range(12)), 128, 192, True, True)
-
-            def d5():
-                tt(o("VP", 256 + lo, 256 + hi), o("VP", 256 + lo, 256 + hi), o("CN", e, z_), A.mult)
-                tt(o("VP", 256 + lo, 256 + hi), o("VP", 256 + lo, 256 + hi), o("ev", lo, hi), A.add)
-                tt(o("wdg", lo, hi), o("wdgw", lo, hi), o("CB", 192 + lo, 192 + hi), A.is_gt)
-                mm(o("TB", W0, W0 + n), o("B16"), o("wdg", lo, hi), True, True)
-                scan(o("sc3", lo, hi), o("RM", lo, hi), o("wdg", lo, hi))
-                tt(lst("ts"), last_lane("sc3"), lst("vmd"), A.mult)
-                tt(o("dn", lo, hi), o("TB", T0, T0 + n), o("gdg", lo, hi), A.mult)
-                tt(lst("ts2"), lst("ts"), o("DL", 12 * t + c0, 12 * t + c1), A.add)
-                tt(o("cR", lo, hi), o("TB", T0 + n, T0 + 2 * n), o("dgS", lo, hi), A.mult)
-                cp(lst("soff"), lst("ts2"))
-                scan(o("sc2", lo, hi), o("RM", lo, hi), o("dn", lo, hi))
-                tt(o("val", lo, hi), o("VP", 256 + lo, 256 + hi), o("cR", lo, hi), A.add)
-                tt(lst("ta"), last_lane("sc1"), lst("vm"), A.mult)
-                cp(ind("Ef", 0, W, lst("soff")), o("val", lo, hi))
-                tt(lst("tb"), lst("ta"), last_lane("sc2"), A.add)
-
-            def d8():
-                tt(lst("tc"), last_lane("sc3"), lst("bmv"), A.mult)
-                tt(lst("vm"), lst("tb"), lst("tc"), A.add)
-                if last:
-                    ts(lst("vfin"), lst("vm"), 1408.0, A.add)
-                else:
-                    ts(lst("voff"), lst("vm"), 1408.0, A.add)
-
-            def d6():
-                WR = o("TB", W0, W0 + n)
-                nl = M + L * t
-                tt(o("VP", 256 + lo, 256 + hi), WR, o("dx", lo, hi), A.mult)
-                tt(o("X", nl + lo, nl + hi), WR, o("x", lo, hi), A.mult)
-                tt(o("x", lo, hi), o("VP", 256 + lo, 256 + hi), o("x", lo, hi), A.add)
-                if not last and lo == 0:
-                    repeat()
-
-            def d7():
-                nl = M + L * t
-                tt(o("capw", lo, hi), o("TB", W0, W0 + n), o("CN", e, z_), A.mult)
-                tt(o("q3", lo, hi), Q1, o("capw", lo, hi), A.mult)
-                act(o("Ef", nl + lo, nl + hi), o("q3", lo, hi), F.Identity, bias=4095.0)
-
-            def d9():
-                cp(lst("vmh"), lst("vm"))
-                ts(lst("vp1"), lst("vm"), 1409.0, A.add)
-            return d1, d2, d3, d4, d5, d6, d7, d8, d9
-
-        AB = batch(0, 128, "S0")
-        C = batch(128, 192, "S1")
-        ssum(2)
-        AB[0]()
-        over(2)
-        act(o("O", 320, 384), o("O", 128, 192), F.Relu, scale=-64.0, bias=192.0)
-        AB[1]()
-        AB[2]()
-        C[0]()
-        mm(o("O", 0, 192), o("Idb"), o("x"), True, False)
-        mm(o("O", 0, 192), o("NegI"), o("yi", L * t, L * t + L), False, True)
-        act(o("xw"), o("O", 0, 192), F.Abs)
-        AB[3]()
-        C[1]()
-        mm(o("O", 0, 192), o("Idb"), o("xw"), True, False)
-        mm(o("O", 0, 192), o("NegI"), o("x"), False, True)
-        act(o("dx"), o("O", 0, 192), F.Copy)
-        for m in range(16):
-            mm(o("O", 384, 396), window("PW1", m), o("xw", m, 192, 16), m == 0, m == 15)
-        C[2]()
-        AB[4]()
-        cp(o("bki"), o("O", 384, 396))
-        ts(o("bka"), o("bki"), 1023, A.bitwise_and)
-        C[3]()
-        ts(o("bkf"), o("bka"), 1.0, A.add)
-        AB[6]()
-        tt(o("bmv"), o("bkf"), o("vp1"), A.subtract)
-        AB[5]()
-        AB[7]()
-        C[4]()
-        C[7]()
-        C[5]()
-        if not last:
-            AB[8]()
+            tb_ = lambda j: o(TB, to[j], to[j] + (n if j < 5 else e1 - e0))
+            xb_ = lambda j: o(XB, xo[j], xo[j] + n)
+            Z, Z17 = o17("Z", c0, c1, 1), o17("Z", c0, c1, 0)
+            capD = o("capD", e0, e1)
+            CN = o("CB", 204 + e0, 204 + e1)
+            tt(capD, Z17, o17("evD", c0, c1, 0), A.is_gt)
+            tt(s("cap"), Z, s("ev"), A.is_gt)
+            scan(o("sc1", 1 + e0, 1 + e1), o("dgv", e0, e1), capD, A.add, A.mult)
+            tt(s("Mc"), Z, s("cap"), A.mult)
+            tt(o("EQd", e0, e1), o("CB", e0, e1), o("sc1", e0, e1), A.is_equal)
+            blocks = range(c0, min(c1, 11))
+            for a in blocks:
+                ts(o("EQ", 204 * a + 17 * a + 17, 204 * a + 204), o("CBh", 17 * a + 17, 204), 1424.0, A.add, o("sc1", 17 * a + 17, 17 * a + 18), A.is_equal)
+            mm([(CN, o("Idb"), o("cK17", e0, e1))] * (bi == 0) + [(CN, o("N18"), capD), (CN, o("PB18"), o("EQd", e0, e1))] +
+               [(o("CB", 204 + 17 * a + 17, 204 + e1), o("PB18"), o("EQ", 204 * a + 17 * a + 17, 204 * a + e1)) for a in blocks if a + 1 < c1], add=bi > 0)
+            scan(o("sc2", e0, e1), CN, o("dgv", e0, e1), A.min, A.max)
+            cp(lst("soff"), o("sc2", e0 + 16, e1, 17))
+            act(o17("nw", c0, c1, 0), CN, F.Sign)
+            if e1 < 204:
+                mm([(o("CB", 204 + e1, 408), o("Idb"), o("cK17", e1, 204))] +
+                   [(o("CB", 204 + e1, 408), o("PB18"), o("EQ", 204 * a + e1, 204 * a + 204)) for a in blocks], more=True)
+            nw = o17("nw", c0, c1, 1)
+            act(s("Wc"), s("Mc"), F.Exp, scale=LN32 / 4096)
+            mm([(tb_(0), o("B16"), s("Wc"))])
+            if CFG["G"][bi] == "S":
+                act(s("Gm"), tb_(0), F.Sign, scale=-1.0, bias=o("thr"))
+            else:
+                ts(s("Gm"), tb_(0), o("thr"), A.is_lt, 2.0, A.mult)
+            mm([(tb_(3), o("Idb"), s("cA")), (tb_(3), o("N18"), s("cap"))])
+            tt(s("a1"), tb_(3), s("ev"), A.add)
+            mm([(tb_(2), o("Idb"), s("cR")), (tb_(2), o("Idb"), o("NC", L * t + lo, L * t + hi)), (tb_(2), o("P18"), s("emp")),
+                (tb_(2), o("P18"), s("cap")), (tb_(2), o("NB2k"), s("Gm"))])
+            tt(s("a2"), tb_(2), s("H"), A.min)
+            tt(ind("Ef", 0, nl + L, lst("soff")), s("a1"), s("a2"), A.max)
+            due(t, "scat%d" % bi)
+            act(s("z1"), Z, F.Copy)
+            mm([(tb_(1), o("Idb"), s("z1")), (tb_(1), o("P16"), s("sig")), (tb_(1), o("N18"), s("emp")), (tb_(1), o("N18"), s("cap"))])
+            act(s("Ws"), tb_(1), F.Exp, scale=SA, bias=o("bk"))
+            mm([(tb_(4), o("BT"), s("Ws"))])
+            tt(o17("sel", c0, c1, 1), tb_(4), s("Ws"), A.is_lt)
+            tt(o17("pay", c0, c1, 1), o17("Z", 12 + c0, 12 + c1, 1), o17("sel", c0, c1, 1), A.mult)
+            mm([(tb_(5), o("N18"), capD), (tb_(5), o("Bo"), o17("sel", c0, c1, 0)), (tb_(5), o("B16"), o17("pay", c0, c1, 0))])
+            scan(o("sc3", e0, e1), o("RM", e0, e1), tb_(5), A.mult, A.max)
+            tt(lst("a3"), o("sc3", e0 + 16, e1, 17), o("sc1", e0 + 17, e1 + 1, 17), A.add)
+            ts(lst("winl"), o("sc2", e0 + 16, e1, 17), nl - 0.5, A.is_lt)
+            tt(lst("tc"), lst("bmv"), lst("winl"), A.mult)
+            tt(lst("vm"), lst("a3"), lst("tc"), A.add)
+            if last:
+                ts(lst("vfin"), lst("vm"), -float(PAD), A.add)
+            else:
+                cp(lst("voff"), lst("vm"))
+                due(t, "voff%d" % bi)
+                ts(lst("vmh"), lst("vm"), -1424.0, A.add)
+            mm([(xb_(0), o("Idb"), yi(lo, hi)), (xb_(0), o("NB18"), nw)])
+            act(s("Yw"), xb_(0), F.Relu, bias=15 * BIG)
+            mm([(xb_(1), o("Idb"), s("x")), (xb_(1), o("NB18"), nw)])
+            act(o("X", nl + lo, nl + hi), xb_(1), F.Relu, bias=15 * BIG)
+            for c in range(3):
+                if CFG["path"][c] == "S" and lo <= CH[c][0] < hi and not last:
+                    turn(c, XB, 0 if bi == 0 else 192, True)
+            mm([(xb_(2), o("Idb"), s("x")), (xb_(2), o("NegI"), s("Yw"))])
+            act(s("x"), xb_(2), F.Abs)
+            due(t, "x%d" % bi)
+            mm([(xb_(3), o("Idb"), s("Mc")), (xb_(3), o("Idb"), s("Cf")), (xb_(3), o("NB18"), nw)])
+            if not last:
+                for c in range(3):
+                    if CFG["path"][c] == "V" and lo <= CH[c][0] < hi:
+                        repeat(*CH[c])
+            if bi == 0:
+                first_new = xb_(3)
+            else:
+                ts(o("Ef", nl, nl + lo), first_new, 1408.0 + 15 * BIG, A.add, 4095.0, A.max)
+                due(t, "new")
+                ts(o("Ef", nl + lo, nl + hi), xb_(3), 1408.0 + 15 * BIG, A.add, 4095.0, A.max)
+                due(t, "new")
         if last:
-            store("Y", T.ykids[:, 0:W - L], o("Ef", 0, W - L))
-            C[6]()
-            store("S", T.ykids[:, W - L:W], o("Ef", W - L, W))
-            store("Y", T.ynodes[:, :], o("X", M, W))
+            store("Y", T.ykids[:, 0:W - L], o("Ef", PAD, nl))
+            store("S", T.ykids[:, W - L:W], o("Ef", nl, nl + L))
+            store("Y", T.ynodes[:, :], o("X", PAD + M, PAD + W))
             store("S", T.ycand[:, :], o("x"))
             store("Y", T.yspot[:, :], o("vfin"))
-        else:
-            deferred.extend((C[8], C[6]))
 
     if "order" not in ORDER:
-        ORDER["order"] = schedule(plan)
+        ORDER["order"] = schedule(plan, dues)
     for i in ORDER["order"]:
         q, calls, reads, writes, kind, _d, _a = plan[i]
         if kind == "x":
@@ -695,8 +663,6 @@ def rank_program(g, core, T, topo):
             before("G", reads)
             calls[0]()
         else:
-            for c in calls[:-1]:
-                emit_now(q, c, reads, writes)
-            emit_now(q, calls[-1], reads, writes, dma=kind == "d")
+            emit_now(q, calls, reads, writes, dma=kind == "d")
     finish()
     g.wait_ge(T.sem.lsem, lcount[0])

@@ -13,7 +13,13 @@ LNB = math.log(1.8)
 CFG = {"path": "VSS", "sign": "VVS", "piece": 2, "xr": "S", "G": "SS", "xn": "SS", "delta": 0.12, "rounds": 1, "ev": ((0, 64), (64, 128), (128, 192)), "tol": 0.1, "bg": 2, "step": 16.0,
        "due": {"offs0": 0.8, "offs64": 1.0, "D0": 3.7, "D1": 5.0, "D2": 7.9, "zq": 4.0, "yi": 8.5, "early": 5.0, "cmp0": 7.7, "cmp1": 9.4, "cmp2": 12.0,
                "scat0": 12.5, "voff0": 13.5, "scat1": 15.8, "x0": 13.5, "sig0": 7.0, "sig1": 8.5, "sig2": 11.0, "new": 19.0}}
-CFG.update({'delta': 0.6, 'tol': 0.15, 'step': 17.0, 'due': {'offs0': 1.55, 'offs64': -2.5, 'D0': 2.45, 'D1': 5.25, 'D2': 7.15, 'zq': 1.5, 'yi': 7.25, 'early': 2.0, 'cmp0': 7.45, 'cmp1': 8.9, 'cmp2': 14.5, 'scat0': 11.75, 'voff0': 16.0, 'scat1': 13.3, 'x0': 15.5, 'sig0': 8.75, 'sig1': 7.75, 'sig2': 14.75, 'new': 17.75, 'offs128': 15.5}})
+CFG.update({'delta': 0.6, 'tol': 0.1, 'step': 17.0, 'rounds': 4, 'mend': 4000, 'heat': 0.3,
+            'due': {'offs0': .8, 'offs64': 1.0, 'offs128': 1.6, 'D0': 3.6, 'D1': 4.6, 'D2': 7.2, 'zq': 3.0, 'yi': 6.5, 'early': 5.0, 'cmp0': 8.1, 'cmp1': 9.7,
+                    'cmp2': 11.6, 'scat0': 13.5, 'voff0': 14.5, 'scat1': 15.5, 'x0': 14.5, 'sig0': 7.5, 'sig1': 9, 'sig2': 11, 'new': 18}})
+CFG.update(step=18.0, bg=2, rounds=6, mend=0, back=30, due={
+    'offs0': 1.0, 'offs64': .9, 'offs128': 3.2, 'xc10': 1.8, 'xc11': 2.55, 'D0': 3.45, 'xc20': 4.2, 'D10': 4.65, 'D11': 5.1, 'xc21': 5.95, 'D20': 6.4,
+    'D21': 7.25, 'zq': 4.5, 'yi': 7.8, 'early': 6.0, 'cmp0': 8.2, 'cmp1': 9.9, 'cmp2': 12.3, 'scat0': 14.5, 'voff0': 15.5, 'scat1': 16, 'x0': 14.6,
+    'sig0': 7.5, 'sig1': 9, 'sig2': 11, 'new': 19})
 
 f32, bf, h16, i32, u16 = "float32", "bfloat16", "float16", "int32", "uint16"
 SCRATCH = {}
@@ -132,7 +138,7 @@ def tracker(g, T):
     return emit, arrive, before, finish
 
 
-WAKE, SELF = 0.10, 0.10
+WAKE, SELF = 0.2, 0.2
 
 
 def schedule(plan, dues):
@@ -168,13 +174,87 @@ def schedule(plan, dues):
     for i in range(n - 1, -1, -1):
         e = min([-level[j] - lat for j, lat in succ[i].items()] + [dues.get(i, NT * CFG["step"] + 3.0)])
         level[i] = -(e - plan[i][5] - (2.0 if plan[i][4] == "d" else 0.0))
+    ORDER["dag"] = (plan, pred, succ, banks)
     best = None
     for _ in range(CFG["rounds"]):
         order, end = one_pass(plan, banks, pred, succ, level)
         if best is None or max(end) < best[0]:
             best = (max(end), order)
-        _o, level = one_pass(plan, banks, succ, pred, end)
-    return best[1]
+        if CFG["rounds"] > 1:
+            _o, level = one_pass(plan, banks, succ, pred, [end[i] - plan[i][5] for i in range(n)])
+    return mend(plan, banks, pred, succ, best[1], sorted(dues))
+
+
+def mend(plan, banks, pred, succ, order, marks):
+    n = len(plan)
+    info = [(p[0], p[4] == "d", p[5], list(pred[i].items()), banks[i]) for i, p in enumerate(plan)]
+
+    def times(order):
+        end, why = [0.0] * n, [None] * n
+        free, last, bank, dfree = {}, {}, {}, 0.0
+        for i in order:
+            q, dma, d, pr, bk = info[i]
+            t, w = (free.get(q, 0.0), (last.get(q), 1)) if q != "X" else (0.0, None)
+            for j, lat in pr:
+                if end[j] + lat >= t:
+                    t, w = end[j] + lat, (j, 0)
+            for b in bk:
+                for q2, j in bank.setdefault(b, {}).items():
+                    if q2 != q and end[j] + WAKE > t:
+                        t, w = end[j] + WAKE, (j, 1)
+                bank[b][q] = i
+            if dma:
+                free[q] = t + 0.1
+                dfree = max(dfree, t + 1.0) + d
+                end[i] = dfree + 1.0
+            else:
+                end[i] = free[q] = t + d
+            last[q], why[i] = i, w
+        return end, why
+    seed = [12345]
+
+    def draw(k):
+        seed[0] = (seed[0] * 1103515245 + 12345) % 2 ** 31
+        return (seed[0] >> 8) % k
+    def cost(end):
+        return max(end) + sum(end[i] for i in marks) / len(marks)
+    end, why = times(order)
+    now = best = cost(end)
+    keep = order
+    for it in range(CFG["mend"]):
+        i, pairs = (marks + [end.index(max(end))])[draw(len(marks) + 1)], []
+        while why[i] is not None and why[i][0] is not None:
+            if why[i][1]:
+                pairs.append((why[i][0], i))
+            i = why[i][0]
+        if not pairs:
+            break
+        a, b = pairs[draw(min(len(pairs), CFG["back"]))]
+        pa, pb = order.index(a), order.index(b)
+        mid = order[pa:pb + 1]
+        if draw(2):
+            move = {b}
+            for j in reversed(mid):
+                if any(k in move for k in succ[j]):
+                    move.add(j)
+            if a in move:
+                continue
+            new = [j for j in mid if j in move] + [j for j in mid if j not in move]
+        else:
+            move = {a}
+            for j in mid:
+                if any(k in move for k in pred[j]):
+                    move.add(j)
+            if b in move:
+                continue
+            new = [j for j in mid if j not in move] + [j for j in mid if j in move]
+        trial = order[:pa] + new + order[pb + 1:]
+        e2, w2 = times(trial)
+        if cost(e2) <= now + CFG["heat"] * (1 - it / CFG["mend"]) * draw(1000) / 1000:
+            order, end, why, now = trial, e2, w2, cost(e2)
+            if now < best:
+                best, keep = now, order
+    return keep
 
 
 def one_pass(plan, banks, pred, succ, level):
@@ -197,10 +277,12 @@ def one_pass(plan, banks, pred, succ, level):
             at[i] = t
         first = min(ready, key=lambda i: (at[i], i))
         near = [i for i in ready if plan[i][0] == plan[first][0] and at[i] <= at[first] + CFG["delta"]]
-        i = max(near, key=lambda i: (round(level[i], 3), -i))
-        fill = [j for j in near if at[j] + plan[j][5] <= at[i] + CFG["tol"] and at[j] < at[i]]
-        if fill:
-            i = max(fill, key=lambda i: (round(level[i], 3), -i))
+        u = max(near, key=lambda i: (round(level[i], 3), -i))
+
+        def late(i, j):
+            return max(at[i] + level[i], max(at[j], at[i] + plan[i][5]) + level[j])
+        fill = [j for j in near if at[j] < at[u] and late(j, u) <= late(u, j) + CFG["tol"]]
+        i = max(fill, key=lambda i: (round(level[i], 3), -i)) if fill else u
         t = at[i]
         ready.remove(i)
         order.append(i)
@@ -232,7 +314,7 @@ def rank_program(g, core, T, topo):
     emit_now, arrive_now, before, finish = tracker(g, T)
     plan = []
     TWO = (bf, h16, u16)
-    CYC, PCYC = 0.001, 0.0005
+    CYC, PCYC = 0.0009, 0.00046
 
     def emit(q, call, reads, writes, dma=False, dur=0.06):
         plan.append((q, [call], reads, writes, "d" if dma else "c", dur, []))
@@ -298,7 +380,7 @@ def rank_program(g, core, T, topo):
             rd_ += lhsT[1] + rhs[1]
             wr_ += out[1]
             dur += PCYC * max(64, rhs[2])
-        mark = [(terms[0][0][3] + "start", 0, 1)]
+        mark = [("start", 0, 1)] if terms[0][0][3] == "CB" else []
         if add and more:
             rd_ += mark + wr_
         elif add:
@@ -422,9 +504,9 @@ def rank_program(g, core, T, topo):
 
     dues = {}
 
-    def due(t, name):
+    def due(t, name, sooner=0.0):
         if name in CFG["due"]:
-            dues[len(plan) - 1] = t * CFG["step"] + CFG["due"][name]
+            dues[len(plan) - 1] = t * CFG["step"] + CFG["due"][name] - sooner
 
     def window(n, k, base=0):
         return o(n, base + 15 - k, base + 143 - k)
@@ -449,7 +531,8 @@ def rank_program(g, core, T, topo):
         act(half("xT", 128 * c, 128 * c + 128), p, F.Abs)
 
     for k in range(16):
-        act(half("Rp", k, 1024, 16), half("NegI", 0, 64), F.Copy)
+        p = half("Rp", k, 1024, 16)
+        act((p[0], [("Rp", k, k + 1)]) + p[2:], half("NegI", 0, 64), F.Copy)
     for c in range(3):
         if CFG["path"][c] == "V":
             repeat(*CH[c])
@@ -474,6 +557,7 @@ def rank_program(g, core, T, topo):
 
     for t in range(NT):
         last = t == NT - 1
+        ORDER.setdefault("starts", {})[t] = len(plan)
         b = T.cores[(r + 1 + t) % N]
         asker = T.cores[(r - 1 - t) % N]
         nl = PAD + M + L * t
@@ -526,7 +610,7 @@ def rank_program(g, core, T, topo):
                 for a in range(lo, hi, w):
                     tt(o3("diff", a, a + w), ind("X", 0, nl, o("offs", a, a + w)), o3("xr", a, a + w), A.subtract)
                     act(o3("D", a, a + w), o3("diff", a, a + w), F.Abs)
-                    due(t, "D%d" % c)
+                    due(t, "D%d" % c, (hi - a - w) / 70.0)
                 if zero_one:
                     ts(o3("sg", lo, hi), o3("diff", lo, hi), 0.0, A.is_le)
                 else:
@@ -535,9 +619,11 @@ def rank_program(g, core, T, topo):
                 for hf, bank in enumerate(("DA", "DB")):
                     a, e = lo + 32 * hf, lo + 32 * hf + 32
                     act(o3("xc", a, e), ind("X", 0, nl, o("offs", a, e)), F.Copy)
-                    mm([(o(bank), half("xT", 128 * c, 128 * c + 128), half("Rp", 512 * hf, 512 * hf + 512)), (o(bank), o("Idb"), o3("xc", a, e))])
+                    due(t, "xc%d%d" % (c, hf))
+                    p = half("Rp", 512 * hf, 512 * hf + 512)
+                    mm([(o(bank), half("xT", 128 * c, 128 * c + 128), (p[0], [("Rp", 0, 16)]) + p[2:]), (o(bank), o("Idb"), o3("xc", a, e))])
                     act(o3("D", a, e), o(bank), F.Abs)
-                    due(t, "D%d" % c)
+                    due(t, "D%d%d" % (c, hf))
                     if zero_one:
                         ts(o3("sg", a, e), o(bank), 0.0, A.is_le)
                     else:
@@ -548,7 +634,7 @@ def rank_program(g, core, T, topo):
             w = (hi - lo) // CFG["bg"]
             for a in range(lo, hi, w):
                 tt(o3("cmp", a, a + w), ind("bk3", 0, books, o("h", a, a + w)), o3("D", a, a + w), A.is_ge)
-                due(t, "cmp%d" % c)
+                due(t, "cmp%d" % c, (hi - a - w) / 40.0)
             mm([(o("O", lo, hi), window("P1s", k), o3("sg", lo, hi, k)) for k in range(16)])
             act(o("sig", lo, hi), o("O", lo, hi), F.Sign, scale=-1.0, bias=9.5 if zero_one else 3.0)
             due(t, "sig%d" % c)

import math
from concourse.bass import DstId, RemoteDMATransfer
from concourse.mybir import AluOpType as A, ActivationFunctionType as F

N = 8
M, L, NT = 2048, 192, 4
W = M + L * NT
PAD = 16
BIG = 2.0 ** 18
C12, C10 = 1.5 * 2.0 ** 19, 1.5 * 2.0 ** 17
LN32 = math.log(32.0)
LNB = math.log(1.8)
CFG = {"path": "VSS", "sign": "VVS", "piece": 2, "xr": "S", "G": "SS", "xn": "SS", "delta": 0.12, "rounds": 1, "ev": ((0, 64), (64, 128), (128, 192)), "tol": 0.1, "bg": 2, "step": 16.0,
       "due": {"offs0": 0.8, "offs64": 1.0, "D0": 3.7, "D1": 5.0, "D2": 7.9, "zq": 4.0, "yi": 8.5, "early": 5.0, "cmp0": 7.7, "cmp1": 9.4, "cmp2": 12.0,
               "scat0": 12.5, "voff0": 13.5, "scat1": 15.8, "x0": 13.5, "sig0": 7.0, "sig1": 8.5, "sig2": 11.0, "new": 19.0}}
CFG.update({'delta': 0.6, 'tol': 0.1, 'step': 17.0, 'rounds': 4, 'mend': 4000, 'heat': 0.3,
            'due': {'offs0': .8, 'offs64': 1.0, 'offs128': 1.6, 'D0': 3.6, 'D1': 4.6, 'D2': 7.2, 'zq': 3.0, 'yi': 6.5, 'early': 5.0, 'cmp0': 8.1, 'cmp1': 9.7,
                    'cmp2': 11.6, 'scat0': 13.5, 'voff0': 14.5, 'scat1': 15.5, 'x0': 14.5, 'sig0': 7.5, 'sig1': 9, 'sig2': 11, 'new': 18}})
CFG.update(step=18.0, bg=2, rounds=6, mend=0, back=30, due={
    'offs0': 1.0, 'offs64': .9, 'offs128': 3.2, 'xc10': 1.8, 'xc11': 2.55, 'D0': 3.45, 'xc20': 4.2, 'D10': 4.65, 'D11': 5.1, 'xc21': 5.95, 'D20': 6.4,
    'D21': 7.25, 'zq': 4.5, 'yi': 7.8, 'early': 6.0, 'cmp0': 8.2, 'cmp1': 9.9, 'cmp2': 12.3, 'scat0': 14.5, 'voff0': 15.5, 'scat1': 16, 'x0': 14.6,
    'sig0': 7.5, 'sig1': 9, 'sig2': 11, 'new': 19})

f32, bf, h16, i32, u16 = "float32", "bfloat16", "float16", "int32", "uint16"
SCRATCH = {}
for _d, _l in (
    (i32, (("kI", M + PAD), ("sp", 12), ("ia", 192), ("ic", 192), ("ic2", 192), ("ib", 128), ("dgi", 192), ("i8", 8), ("p0", 1), ("p1", 1), ("p2", 1),
           ("i17", 204), ("j17", 204), ("nci", 768), ("dli", 48), ("ev", 192), ("Ci", 192), ("Pi", 256), ("Pd", 256))),
    (f32, (("Ef", W + PAD), ("pm", 1), ("pb", 1), ("bk", 1), ("thr", 1), ("dgF", 192), ("H", 192), ("evD", 192), ("dgv", 204), ("sc1", 208), ("sc2", 204),
           ("sc3", 204), ("b1", 12), ("bmv", 12), ("a1", 192), ("a2", 192), ("u1s", 256), ("He", 256), ("a3", 12), ("winl", 12), ("tc", 12), ("vm", 12), ("vfin", 12))),
    (bf, (("X", W + PAD), ("bk3", 6144), ("x", 192), ("wt", 2), ("cK", 192), ("cA", 192), ("cR", 192), ("dg17", 204), ("cK17", 204), ("RM", 204),
          ("c89", 204), ("c12", 128), ("cZ", 68), ("z1", 192), ("xT", 384), ("Rp", 1024), ("Idb", 128), ("NegI", 128), ("N18", 128), ("P18", 128), ("N16", 128), ("P16", 128),
          ("B16", 128), ("NB18", 128), ("PB18", 128), ("BT", 128), ("NB2k", 128), ("Bo", 128), ("G8", 8), ("Sm", 2048),
          ("PW1", 143), ("PW2", 143), ("P1s", 143), ("P4s", 143), ("FP", 8 * 144), ("emp", 192), ("sig", 192), ("cap", 192), ("Mc", 192),
          ("Wc", 192), ("Ws", 192), ("Gm", 192), ("sel", 192), ("EQ", 12 * 204), ("EQd", 204), ("zd", 192), ("z", 192), ("xw", 192), ("Yw", 192),
          ("t2", 512), ("tb", 12), ("wf", 2 * NT), ("yo", L * NT), ("yi", L * NT))),
    (h16, (("NC", 768), ("DLh", 48), ("c122", 12), ("vmh", 12), ("Cf", 192), ("CBh", 204), ("pay", 192))),
    (u16, (("voff", 12), ("soff", 12), ("offs", 192), ("h", 192), ("zq", 12 * NT), ("qi", 12 * NT))),
):
    for _n, _w in _l:
        SCRATCH[_n] = ("sbuf", [128, _w], _d)
for _n in ("xr", "xc", "diff", "D", "sg", "cmp"):
    SCRATCH[_n] = ("sbuf", [128, 3072], bf)
SCRATCH["capD"] = ("sbuf", [128, 204], bf)
SCRATCH["evD"] = ("sbuf", [128, 12, 17], f32)
SCRATCH["pay"] = ("sbuf", [128, 12, 17], h16)
for _n in ("nw", "sel"):
    SCRATCH[_n] = ("sbuf", [128, 12, 17], bf)
PSUM = ["DA", "DB", "U0", "U1", "O", "Z", "CB", "TB"]
for _n in PSUM:
    SCRATCH[_n] = ("psum", [128, 512] if _n != "Z" else [128, 30, 17], f32)
NDMA = 16
SEMAPHORES = ["sV", "sS", "sP", "sG", "lsem", "wa"] + ["qa%d" % t for t in range(NT)] + ["ra%d" % t for t in range(NT)] + ["d%d" % i for i in range(NDMA)]


def tracker(g, T):
    eng = {"V": g.vector, "S": g.scalar, "P": g.tensor, "G": g, "Y": g.sync}
    know = {q: {} for q in eng}
    cnt = {q: 0 for q in eng}
    wr, rd, bank, used = {}, {}, {}, [0]

    def waits(q, ops):
        k = know[q]
        ops = [o for o in ops if k.get(o[0], 0) < o[1]]
        ops.sort(key=lambda o: -len(o[2]))
        best = {}
        for o in ops:
            if o[0] not in best or best[o[0]][1] < o[1]:
                best[o[0]] = o
        ops = list(best.values())
        keep = []
        for o in ops:
            if not any(p is not o and p[2].get(o[0], 0) >= o[1] for p in ops):
                keep.append(o)
        for o in keep:
            eng[q].wait_ge(T.sem[o[0]], o[1])
        for o in keep:
            for s, v in o[2].items():
                if k.get(s, 0) < v:
                    k[s] = v

    def deps(q, reads, writes, dma):
        out = []
        for n, lo, hi in reads:
            out += [o for a, b, o in wr.get(n, []) if a < hi and lo < b]
        for n, lo, hi in writes:
            for a, b, o in wr.get(n, []):
                if a < hi and lo < b and not (o[3] == q == "P"):
                    out.append(o)
            for a, b, o in rd.get(n, []):
                if a < hi and lo < b and (o[3] != q or dma):
                    out.append(o)
        for n in set([r[0] for r in reads + writes]):
            if n in PSUM:
                out += [o for p, o in bank.get(n, {}).items() if p != q]
        if q == "P":
            out = [o for o in out if o[3] != "P"]
        return out

    def note(op, reads, writes, q):
        for n, lo, hi in writes:
            wr[n] = [e for e in wr.get(n, []) if not (lo <= e[0] and e[1] <= hi)] + [(lo, hi, op)]
            rd[n] = [e for e in rd.get(n, []) if not (lo <= e[0] and e[1] <= hi)]
        for n, lo, hi in reads:
            old = [e for e in rd.get(n, []) if not (lo <= e[0] and e[1] <= hi and e[2][3] == q and op[4] == 0 and e[2][4] == 0)]
            rd[n] = old + [(lo, hi, op)]
        for n in set([r[0] for r in reads + writes]):
            if n in PSUM:
                bank.setdefault(n, {})[q] = op

    def emit(q, calls, reads, writes, dma=False):
        waits(q, deps(q, reads, writes, dma))
        for call in calls:
            ins = call(eng[q])
        if dma:
            s, v = "d%d" % used[0], 16
            used[0] += 1
        else:
            cnt[q] += 1
            s, v = "s" + q, cnt[q]
        ins.then_inc(T.sem[s], 16 if dma else 1)
        clk = dict(know[q])
        clk[s] = v
        note((s, v, clk, "d" if dma else q, 1 if dma else 0), reads, writes, q)

    def arrive(sem, val, name, lo, hi):
        note((sem, val, {sem: val}, "X", 1), [], [(name, lo, hi)], "X")

    def before(q, reads):
        waits(q, deps(q, reads, [], True))

    def finish():
        for q in eng:
            if cnt[q]:
                g.wait_ge(T.sem["s" + q], cnt[q])
        for i in range(used[0]):
            g.wait_ge(T.sem["d%d" % i], 16)
    return emit, arrive, before, finish


WAKE, SELF = 0.2, 0.2


def schedule(plan, dues):
    n = len(plan)
    pred = [{} for _ in range(n)]
    succ = [{} for _ in range(n)]
    wr, rd = {}, {}

    def edge(a, b, lat):
        if a != b and pred[b].get(a, -1.0) < lat:
            pred[b][a] = lat
            succ[a][b] = lat
    for i, (q, _c, reads, writes, kind, _d, after) in enumerate(plan):
        for j in after:
            edge(j, i, 0.0)
            if kind == "d":
                pred[i][j] = succ[j][i] = -50.0
        for b, lo, hi in reads:
            for x, y, j in wr.get(b, []):
                if x < hi and lo < y:
                    edge(j, i, WAKE if plan[j][0] != q or kind == "d" else 0.0 if q == "P" else SELF)
        for b, lo, hi in writes:
            for x, y, j in wr.get(b, []) + rd.get(b, []):
                if x < hi and lo < y:
                    edge(j, i, WAKE if plan[j][0] != q else 0.0)
        for b, lo, hi in writes:
            wr[b] = [e for e in wr.get(b, []) if not (lo <= e[0] and e[1] <= hi)] + [(lo, hi, i)]
            rd[b] = [e for e in rd.get(b, []) if not (lo <= e[0] and e[1] <= hi)]
        for b, lo, hi in reads:
            rd.setdefault(b, []).append((lo, hi, i))
    level = [0.0] * n
    banks = [sorted(set(b for b, _l, _h in p[2] + p[3] if b in PSUM)) for p in plan]
    for i in range(n - 1, -1, -1):
        e = min([-level[j] - lat for j, lat in succ[i].items()] + [dues.get(i, NT * CFG["step"] + 3.0)])
        level[i] = -(e - plan[i][5] - (2.0 if plan[i][4] == "d" else 0.0))
    ORDER["dag"] = (plan, pred, succ, banks)
    best = None
    for _ in range(CFG["rounds"]):
        order, end = one_pass(plan, banks, pred, succ, level)
        if best is None or max(end) < best[0]:
            best = (max(end), order)
        if CFG["rounds"] > 1:
            _o, level = one_pass(plan, banks, succ, pred, [end[i] - plan[i][5] for i in range(n)])
    return mend(plan, banks, pred, succ, best[1], sorted(dues))


def mend(plan, banks, pred, succ, order, marks):
    n = len(plan)
    info = [(p[0], p[4] == "d", p[5], list(pred[i].items()), banks[i]) for i, p in enumerate(plan)]

    def times(order):
        end, why = [0.0] * n, [None] * n
        free, last, bank, dfree = {}, {}, {}, 0.0
        for i in order:
            q, dma, d, pr, bk = info[i]
            t, w = (free.get(q, 0.0), (last.get(q), 1)) if q != "X" else (0.0, None)
            for j, lat in pr:
                if end[j] + lat >= t:
                    t, w = end[j] + lat, (j, 0)
            for b in bk:
                for q2, j in bank.setdefault(b, {}).items():
                    if q2 != q and end[j] + WAKE > t:
                        t, w = end[j] + WAKE, (j, 1)
                bank[b][q] = i
            if dma:
                free[q] = t + 0.1
                dfree = max(dfree, t + 1.0) + d
                end[i] = dfree + 1.0
            else:
                end[i] = free[q] = t + d
            last[q], why[i] = i, w
        return end, why
    seed = [12345]

    def draw(k):
        seed[0] = (seed[0] * 1103515245 + 12345) % 2 ** 31
        return (seed[0] >> 8) % k
    def cost(end):
        return max(end) + sum(end[i] for i in marks) / len(marks)
    end, why = times(order)
    now = best = cost(end)
    keep = order
    for it in range(CFG["mend"]):
        i, pairs = (marks + [end.index(max(end))])[draw(len(marks) + 1)], []
        while why[i] is not None and why[i][0] is not None:
            if why[i][1]:
                pairs.append((why[i][0], i))
            i = why[i][0]
        if not pairs:
            break
        a, b = pairs[draw(min(len(pairs), CFG["back"]))]
        pa, pb = order.index(a), order.index(b)
        mid = order[pa:pb + 1]
        if draw(2):
            move = {b}
            for j in reversed(mid):
                if any(k in move for k in succ[j]):
                    move.add(j)
            if a in move:
                continue
            new = [j for j in mid if j in move] + [j for j in mid if j not in move]
        else:
            move = {a}
            for j in mid:
                if any(k in move for k in pred[j]):
                    move.add(j)
            if b in move:
                continue
            new = [j for j in mid if j not in move] + [j for j in mid if j in move]
        trial = order[:pa] + new + order[pb + 1:]
        e2, w2 = times(trial)
        if cost(e2) <= now + CFG["heat"] * (1 - it / CFG["mend"]) * draw(1000) / 1000:
            order, end, why, now = trial, e2, w2, cost(e2)
            if now < best:
                best, keep = now, order
    return keep


def one_pass(plan, banks, pred, succ, level):
    n = len(plan)
    left = [len(p) for p in pred]
    end = [0.0] * n
    early = [0.0] * n
    free, bank, dfree = {}, {}, 0.0
    ready = [i for i in range(n) if left[i] == 0]
    order = []
    while ready:
        at = {}
        for i in ready:
            q = plan[i][0]
            t = max(early[i], free.get(q, 0.0)) if q != "X" else early[i]
            for b in banks[i]:
                for q2, e in bank.get(b, {}).items():
                    if q2 != q and e + WAKE > t:
                        t = e + WAKE
            at[i] = t
        first = min(ready, key=lambda i: (at[i], i))
        near = [i for i in ready if plan[i][0] == plan[first][0] and at[i] <= at[first] + CFG["delta"]]
        u = max(near, key=lambda i: (round(level[i], 3), -i))

        def late(i, j):
            return max(at[i] + level[i], max(at[j], at[i] + plan[i][5]) + level[j])
        fill = [j for j in near if at[j] < at[u] and late(j, u) <= late(u, j) + CFG["tol"]]
        i = max(fill, key=lambda i: (round(level[i], 3), -i)) if fill else u
        t = at[i]
        ready.remove(i)
        order.append(i)
        q, kind, d = plan[i][0], plan[i][4], plan[i][5]
        if kind == "d":
            free[q] = t + 0.1
            dfree = max(dfree, t + 1.0) + d
            end[i] = dfree + 1.0
        else:
            end[i] = t + d
            free[q] = end[i]
        for b in banks[i]:
            bank.setdefault(b, {})[q] = end[i]
        for j, lat in succ[i].items():
            early[j] = max(early[j], end[i] + lat)
            left[j] -= 1
            if left[j] == 0:
                ready.append(j)
    return order, end


ORDER = {}


def rank_program(g, core, T, topo):
    r = T.rank_of(core)
    if r is None:
        return
    emit_now, arrive_now, before, finish = tracker(g, T)
    plan = []
    TWO = (bf, h16, u16)
    CYC, PCYC = 0.0009, 0.00046

    def emit(q, call, reads, writes, dma=False, dur=0.06):
        plan.append((q, [call], reads, writes, "d" if dma else "c", dur, []))

    def o(n, lo=0, hi=None, step=1):
        hi = SCRATCH[n][1][1] if hi is None else hi
        return (T[n][:, lo:hi] if step == 1 else T[n][:, lo:hi:step], [(n, lo, hi)], (hi - lo + step - 1) // step, n, False)

    def o3(n, lo, hi, k=None):
        ap = T[n][:, 16 * lo:16 * hi] if k is None else T[n][:, 16 * lo + k:16 * hi:16]
        names = [n] if n != "xr" else ["xr%d" % j for j in (range(16) if k is None else [k])]
        return (ap, [(m, lo, hi) for m in names], (hi - lo) * (16 if k is None else 1), n, False)

    def o17(n, c0, c1, k0):
        return (T[n][:, c0:c1, k0:17], [(n, 17 * c0, 17 * c1)], (c1 - c0) * (17 - k0), n, False)

    def ind(n, lo, hi, off):
        return (T[n][:, lo:hi].indirect(off[0]), [(n, lo, hi)] + off[1], 16 * off[2], n, True)

    def sca(s):
        return (s[0], s[1]) if isinstance(s, tuple) else (s, [])

    def time_of(out, a, b=None):
        if a[4]:
            return 0.06 + 1.56 * CYC * out[2]
        if out[4]:
            return 0.06 + 3.8 * CYC * out[2]
        if b is not None:
            f = 1.0 if a[3] in PSUM or b[3] in PSUM else 2.0
        else:
            f = 0.5 if SCRATCH[a[3]][2] in TWO and SCRATCH[out[3]][2] in TWO else 1.0
        return CYC * max(64, f * out[2])

    def tt(out, a, b, op):
        rd_, wr_ = (out[1][1:], out[1][:1]) if out[4] else ([], out[1])
        emit("V", lambda e: e.tensor_tensor(out[0], a[0], b[0], op), a[1] + b[1] + rd_, wr_, dur=time_of(out, a, b))

    def ts(out, a, s1, op0, s2=None, op1=None):
        s1, s2 = sca(s1), sca(s2)
        if op1 is None:
            emit("V", lambda e: e.tensor_scalar(out[0], a[0], s1[0], None, op0), a[1] + s1[1], out[1], dur=time_of(out, a))
        else:
            emit("V", lambda e: e.tensor_scalar(out[0], a[0], s1[0], s2[0], op0, op1), a[1] + s1[1] + s2[1], out[1], dur=time_of(out, a))

    def cp(out, a):
        emit("V", lambda e: e.tensor_copy(out[0], a[0]), a[1], out[1], dur=time_of(out, a))

    def ms(out, c):
        emit("V", lambda e: e.memset(out[0], c), [], out[1], dur=time_of(out, out))

    def scan(out, a, b, op0, op1):
        emit("V", lambda e: e.tensor_tensor_scan(out[0], a[0], b[0], 0.0, op0, op1), a[1] + b[1], out[1], dur=CYC * max(64, out[2]))

    def act(out, a, func, scale=1.0, bias=0.0):
        s, b = sca(scale), sca(bias)
        emit("S", lambda e: e.activation(out[0], a[0], func, bias=b[0], scale=s[0]), a[1] + s[1] + b[1], out[1],
             dur=0.065 + CYC * out[2] * 1.56 if a[4] else CYC * max(64, out[2]))

    def mm(terms, add=False, more=False):
        calls, rd_, wr_, dur = [], [], [], 0.0
        for i, (out, lhsT, rhs) in enumerate(terms):
            calls.append(lambda e, out=out, lhsT=lhsT, rhs=rhs, i=i: e.matmul(out[0], lhsT[0], rhs[0], i == 0 and not add, i == len(terms) - 1 and not more))
            rd_ += lhsT[1] + rhs[1]
            wr_ += out[1]
            dur += PCYC * max(64, rhs[2])
        mark = [("start", 0, 1)] if terms[0][0][3] == "CB" else []
        if add and more:
            rd_ += mark + wr_
        elif add:
            rd_ += wr_
            wr_ += mark
        else:
            wr_ += mark
        plan.append(("P", calls, sorted(set(rd_)), sorted(set(wr_)), "c", dur, []))

    def iota(n, pattern, base, cm):
        b = o(n)
        emit("G", lambda e: e.iota(b[0], pattern, base, cm), [], b[1], dur=0.15 + 2 * CYC * b[2])

    def load(q, name, lo, hi, src):
        b = o(name, lo, hi)
        emit(q, lambda e: e.dma_start(b[0], src), [], b[1], dma=True, dur=0.0013 * b[2] * (1 if SCRATCH[name][2] in TWO else 2))

    def store(q, dst, b):
        emit(q, lambda e: e.dma_start(dst, b[0]), b[1], [], dma=True, dur=0.0013 * b[2] * (1 if SCRATCH[b[3]][2] in TWO else 2))

    load("S", "wt", 0, 2, T.wts[:, :])
    load("Y", "sp", 0, 12, T.spot[:, :])
    load("Y", "kI", PAD, M + PAD, T.kids[:, :])
    load("S", "x", 0, 192, T.cand[:, :])
    load("Y", "X", PAD, M + PAD, T.nodes[:, :])
    for j in range(3):
        load("Y", "bk3", 2048 * j, 2048 * j + 2048, T.book[:, :])
    loads = [i for i in range(len(plan)) if plan[i][0] == "Y"]
    for a_, b_ in zip(loads, loads[1:]):
        plan[a_][3].append(("ld%d" % b_, 0, 0))
        plan[b_][6].append(a_)

    iota("p0", [[0, 1]], 0, 1)
    iota("ia", [[1, 192]], 1024, -1)
    iota("ic", [[1, 192]], 0, 0)
    iota("i8", [[1, 8]], 0, 0)
    iota("i17", [[0, 12], [1, 17]], 1023, -1)
    iota("dli", [[16, 48]], M + PAD - 1424, 0)
    iota("nci", [[1, 768]], 0, 0)

    allto = [T.cores[(r - 1 - t) % N] for t in range(NT)]
    common = [e for e in topo.engines(core, allto[0]) if all(e in topo.engines(core, c) for c in allto)][:8]
    wmask = sum(1 << e for e in common)
    lcount = [0]

    def send_weights():
        g.remote_dma_fused([RemoteDMATransfer(
            dst_ids=[DstId(rid=topo.addr(c)[0], pnc=topo.addr(c)[1]) for c in allto], dma_engine_mask=wmask,
            remote_sem=T.sem.wa, srcs=[T.wt[:, :]], dsts=[T.wf[:, 2 * t:2 * t + 2] for t in range(NT)])], local_sem=T.sem.lsem)
        lcount[0] += len(common)

    def arrive(sem, val, name, lo, hi, lat):
        plan.append(("X", [lambda: arrive_now(sem, val, name, lo, hi)], [], [(name, lo, hi)], "x", lat, [sends[-1]]))

    sends = [len(plan)]
    plan.append(("G", [send_weights], [("wt", 0, 2)], [], "s", 1.0, []))
    arrive("wa", len(common) * NT, "wf", 0, 2 * NT, 4.0)

    def send(dst, out_n, in_n, lo, hi, sem):
        eng = topo.engines(core, dst)[:8]
        rid, pid, _s = topo.addr(dst)

        def call():
            g.remote_dma(T[out_n][:, lo:hi], T[in_n][:, lo:hi], T.sem[sem], T.sem.lsem, pid, rid, sum(1 << e for e in eng))
            lcount[0] += len(eng)
        sends.append(len(plan))
        plan.append(("G", [call], [(in_n, lo, hi)], [], "s", 1.0, []))

    ms(o("X", 0, PAD), 512.0)
    ms(o("kI", 0, PAD), 0)
    ms(o("Ef", 0, PAD), 0.0)
    for n in ("PW1", "PW2", "P1s", "P4s"):
        ms(o(n), 0.0)
    for t in range(NT):
        ms(o("FP", 288 * t, 288 * t + 288), 0.0)
    for n, c in (("c89", 89.0), ("c12", C12), ("cZ", -65536.0)):
        ms(o(n), c)
    ms(o("sc1", 0, 4), 0.0)
    ms(o17("evD", 0, 12, 0), BIG)
    ts(o("voff"), o("sp"), float(PAD), A.add)
    ts(o("vmh"), o("sp"), -1408.0, A.add)
    ts(o("p1"), o("p0"), 15, A.bitwise_and)
    cp(o("pm"), o("p1"))
    ts(o("p2"), o("p0"), 4, A.arith_shift_right)
    cp(o("pb"), o("p2"))
    ts(o("c122"), o("c89", 0, 12), 0.0, A.mult, (C10 - 1408.0) / 16, A.add)
    ts(o("dgi"), o("ia"), 15, A.bitwise_and)
    ts(o("dgF"), o("dgi"), 0.0, A.is_equal)
    act(o("cK"), o("dgF"), F.Identity, scale=BIG, bias=-BIG)
    act(o("cA"), o("dgF"), F.Identity, scale=PAD - BIG, bias=-float(PAD))
    act(o("cR"), o("dgF"), F.Identity, scale=-4096.0, bias=M + 32768.0 + 4096.0 - BIG)
    act(o("H"), o("dgF"), F.Identity, scale=BIG - 4095.0, bias=4095.0)
    ts(o("Idb"), o("ia", 0, 128), 1024.0, A.is_equal)
    ts(o("ib"), o("ic", 0, 128), 4, A.arith_shift_right)
    ts(o("B16"), o("ib"), o("pb"), A.is_equal)
    for n, c in (("NegI", -1.0), ("N18", -BIG), ("P18", BIG), ("N16", -65536.0), ("P16", 65536.0)):
        act(o(n), o("Idb"), F.Copy, scale=c)
    for n, c in (("NB18", -BIG), ("PB18", BIG), ("BT", 0.4), ("NB2k", -2048.0), ("Bo", 1424.0)):
        act(o(n), o("B16"), F.Copy, scale=c)
    ts(o("G8"), o("i8"), o("pb"), A.is_equal)
    ts(o("P1s", 15, 143, 16), o("G8"), 1.0, A.mult)
    ts(o("P4s", 15, 143, 16), o("G8"), 4096.0, A.mult)
    ts(o("PW1", 15, 143, 16), o("G8"), o("wt", 0, 1), A.mult)
    ts(o("PW2", 15, 143, 16), o("G8"), o("wt", 1, 2), A.mult)
    ms(o("RM"), 1.0)
    ms(o("RM", 0, 204, 17), 0.0)
    ms(o17("sel", 0, 12, 0), 0.0)
    ms(o17("pay", 0, 12, 0), 0.0)
    for m in range(16):
        act(o("Sm", 128 * m, 128 * m + 128), o("B16"), F.Copy, scale=o("dgF", m, m + 1))
    ts(o("j17"), o("i17"), 15, A.bitwise_and)
    ts(o("dg17"), o("j17"), 0.0, A.is_equal)
    act(o("cK17"), o("dg17"), F.Identity, scale=-BIG, bias=2 * BIG)
    ms(o("cK17", 0, 204, 17), 2 * BIG)
    ms(o("dg17", 0, 204, 17), 1.0)
    ts(o("DLh"), o("dli"), o("pm"), A.add)
    cp(o("NC"), o("nci"))
    SA = 16 * LNB / 4096
    act(o("bk"), o("pm"), F.Identity, scale=-LNB, bias=15 * LNB - 79.3 + 65536.0 * SA)
    act(o("thr"), o("pm"), F.Exp, scale=LN32, bias=math.log(24.0))

    dues = {}

    def due(t, name, sooner=0.0):
        if name in CFG["due"]:
            dues[len(plan) - 1] = t * CFG["step"] + CFG["due"][name] - sooner

    def window(n, k, base=0):
        return o(n, base + 15 - k, base + 143 - k)

    def repeat(lo, hi):
        for k in range(16):
            if CFG["xr"] == "S":
                act(o3("xr", lo, hi, k), o("x", lo, hi), F.Copy)
            else:
                cp(o3("xr", lo, hi, k), o("x", lo, hi))

    CH = ((0, 64), (64, 128), (128, 192))
    UB = ("U0", "U1", "U0")

    def half(n, lo, hi, step=1):
        x_ = o(n, lo, hi, step)
        return (T[n][0:64, lo:hi] if step == 1 else T[n][0:64, lo:hi:step],) + x_[1:]

    def turn(c, bank, at, less):
        p = half(bank, at, at + 128)
        mm([(p, o("x", *CH[c]), o("Idb"))] + ([(p, o("Yw", *CH[c]), o("NegI"))] if less else []))
        act(half("xT", 128 * c, 128 * c + 128), p, F.Abs)

    for k in range(16):
        p = half("Rp", k, 1024, 16)
        act((p[0], [("Rp", k, k + 1)]) + p[2:], half("NegI", 0, 64), F.Copy)
    for c in range(3):
        if CFG["path"][c] == "V":
            repeat(*CH[c])
        else:
            turn(c, "TB", 128 * c, False)

    def hash_(U, n, w, out, once):
        c = (64 * w, 64 * w + n)
        u2 = o(U, n, 2 * n)
        act(o("t2", 128 * w, 128 * w + 2 * n), o(U, 0, 2 * n), F.Identity, bias=-2047.5)
        tt(o("u1s", *c), o(U, 0, n), o("t2", 128 * w, 128 * w + n), A.subtract)
        tt(u2, u2, o("t2", 128 * w + n, 128 * w + 2 * n), A.subtract)
        tt(o("Pi", *c), o("u1s", *c), u2, A.mult)
        ts(o("Pd", *c), o("Pi", *c), 5, A.arith_shift_right, 2047, A.bitwise_and)
        if once:
            tt(o("Pi", *c), o("Pd", *c), u2, A.add)
            ts(o("Pd", *c), o("Pi", *c), 2047, A.bitwise_and)
            cp(out, o("Pd", *c))
        else:
            tt(o("He", *c), o("Pd", *c), u2, A.add)
            cp(out, o("He", *c))

    for t in range(NT):
        last = t == NT - 1
        ORDER.setdefault("starts", {})[t] = len(plan)
        b = T.cores[(r + 1 + t) % N]
        asker = T.cores[(r - 1 - t) % N]
        nl = PAD + M + L * t
        books = 2048 if t == 0 else 6144
        stood = PAD + M + L * max(t - 1, 0)

        for lo, hi in CFG["ev"]:
            ts(o("ev", lo, hi), ind("kI" if t == 0 else "Ef", 0, stood, o("voff", lo // 16, hi // 16)), float(PAD), A.add)
            ts(o("Ci", lo, hi), o("ev", lo, hi), 4095, A.bitwise_and)
            cp(o("offs", lo, hi), o("Ci", lo, hi))
            due(t, "offs%d" % lo)
        if t == 0:
            for j in range(4):
                cp(o("Ef", PAD + 512 * j, PAD + 512 * j + 512), o("kI", PAD + 512 * j, PAD + 512 * j + 512))
        for j in range(2 * t, 2 * t + 2):
            ts(o("FP", 144 * j + 15, 144 * j + 143, 16), o("G8"), o("wf", j, j + 1), A.mult)

        tt(o("zd"), ind("X", 0, stood, o("voff")), o("x"), A.subtract)
        act(o("z"), o("zd"), F.Abs)
        mm([(o("U1", 0, 24), o("Idb"), o("c12", 0, 24))] +
           [(o("U1", 12 * j, 12 * j + 12), window("FP", m, 144 * (2 * t + j)), o("z", m, 192, 16)) for j in range(2) for m in range(16)])
        hash_("U1", 12, 3, o("zq", 12 * t, 12 * t + 12), t == 0)
        due(t, "zq")
        send(b, "qi", "zq", 12 * t, 12 * t + 12, "qa%d" % t)
        arrive("qa%d" % t, len(topo.engines(asker, core)[:8]), "qi", 12 * t, 12 * t + 12, 2.0)
        act(o("yo", L * t, L * t + L), ind("bk3", 0, books, o("qi", 12 * t, 12 * t + 12)), F.Copy)
        due(t, "yi")
        send(asker, "yi", "yo", L * t, L * t + L, "ra%d" % t)
        arrive("ra%d" % t, len(topo.engines(b, core)[:8]), "yi", L * t, L * t + L, 3.0)

        ts(o("emp"), o("offs"), float(PAD - 1), A.is_equal)
        ts(o("Cf"), o("offs"), -1424.0, A.add)
        mm([(o("O", 192, 384), o("Idb"), o("cK")), (o("O", 192, 384), o("N18"), o("emp"))])
        tt(o17("evD", 0, 12, 1), o("O", 192, 384), o("ev"), A.add)
        due(t, "early")
        mm([(o17("Z", 12, 24, 1), o("Idb"), o("Cf"))])
        mm([(o("CB", 0, 204), o("B16"), o("c89"))] +
           [(o("CB", 1 + m, 204, 17), o("Sm", 128 * m, 128 * m + 128), o("vmh")) for m in range(16)] +
           [(o("CB", 0, 204, 17), o("Idb"), o("DLh", 12 * t, 12 * t + 12))])
        ts(o("CBh", 17, 204), o("CB", 17, 204), -1424.0, A.add)
        due(t, "early")
        tt(o("dgv"), o("CB", 0, 204), o("dg17"), A.mult)
        due(t, "early")

        for c, (lo, hi) in enumerate(CH):
            U = UB[c]
            zero_one = CFG["sign"][c] == "V"
            if CFG["path"][c] == "V":
                w = (hi - lo) // CFG["piece"]
                for a in range(lo, hi, w):
                    tt(o3("diff", a, a + w), ind("X", 0, nl, o("offs", a, a + w)), o3("xr", a, a + w), A.subtract)
                    act(o3("D", a, a + w), o3("diff", a, a + w), F.Abs)
                    due(t, "D%d" % c, (hi - a - w) / 70.0)
                if zero_one:
                    ts(o3("sg", lo, hi), o3("diff", lo, hi), 0.0, A.is_le)
                else:
                    act(o3("sg", lo, hi), o3("diff", lo, hi), F.Sign, scale=-1.0, bias=0.5)
            else:
                for hf, bank in enumerate(("DA", "DB")):
                    a, e = lo + 32 * hf, lo + 32 * hf + 32
                    act(o3("xc", a, e), ind("X", 0, nl, o("offs", a, e)), F.Copy)
                    due(t, "xc%d%d" % (c, hf))
                    p = half("Rp", 512 * hf, 512 * hf + 512)
                    mm([(o(bank), half("xT", 128 * c, 128 * c + 128), (p[0], [("Rp", 0, 16)]) + p[2:]), (o(bank), o("Idb"), o3("xc", a, e))])
                    act(o3("D", a, e), o(bank), F.Abs)
                    due(t, "D%d%d" % (c, hf))
                    if zero_one:
                        ts(o3("sg", a, e), o(bank), 0.0, A.is_le)
                    else:
                        act(o3("sg", a, e), o(bank), F.Sign, scale=-1.0, bias=0.5)
            mm([(o(U, 0, 128), o("Idb"), o("c12"))] +
               [(o(U, 64 * j, 64 * j + 64), window("PW%d" % (j + 1), k), o3("D", lo, hi, k)) for j in range(2) for k in range(16)])
            hash_(U, 64, c, o("h", lo, hi), t == 0)
            w = (hi - lo) // CFG["bg"]
            for a in range(lo, hi, w):
                tt(o3("cmp", a, a + w), ind("bk3", 0, books, o("h", a, a + w)), o3("D", a, a + w), A.is_ge)
                due(t, "cmp%d" % c, (hi - a - w) / 40.0)
            mm([(o("O", lo, hi), window("P1s", k), o3("sg", lo, hi, k)) for k in range(16)])
            act(o("sig", lo, hi), o("O", lo, hi), F.Sign, scale=-1.0, bias=9.5 if zero_one else 3.0)
            due(t, "sig%d" % c)
            Z = o17("Z", lo // 16, hi // 16, 1)
            mm([(o17("Z", lo // 16, hi // 16, 0), o("Idb"), o("cZ")), (Z, o("N16"), o("sig", lo, hi))] +
               [(Z, window("P4s", k), o3("cmp", lo, hi, k)) for k in range(16)])

        yi = lambda lo, hi: o("yi", L * t + lo, L * t + hi)
        mm([(o("O", 192, 384), o("Idb"), o("x")), (o("O", 192, 384), o("NegI"), yi(0, L))])
        act(o("xw"), o("O", 192, 384), F.Abs)
        mm([(o("U1", 0, 12), o("B16"), o("c122"))] + [(o("U1", 0, 12), window("PW1", m), o("xw", m, 192, 16)) for m in range(16)])
        act(o("tb"), o("U1", 0, 12), F.Identity, bias=1408.0 - 511.5)
        tt(o("b1"), o("U1", 0, 12), o("tb"), A.subtract)
        tt(o("bmv"), o("b1"), o("vmh"), A.subtract)

        for bi, (lo, hi, TB, to, XB, xo) in enumerate(((0, 128, "TB", (0, 128, 256, 384, 384, 0), "DB", (0, 128, 256, 384)),
                                                       (128, 192, "DA", (0, 64, 128, 192, 256, 320), "O", (0, 64, 128, 384)))):
            n = hi - lo
            c0, c1 = lo // 16, hi // 16
            e0, e1 = 17 * c0, 17 * c1
            s = lambda nm: o(nm, lo, hi)
            lst = lambda nm: o(nm, c0, c1)
            tb_ = lambda j: o(TB, to[j], to[j] + (n if j < 5 else e1 - e0))
            xb_ = lambda j: o(XB, xo[j], xo[j] + n)
            Z, Z17 = o17("Z", c0, c1, 1), o17("Z", c0, c1, 0)
            capD = o("capD", e0, e1)
            CN = o("CB", 204 + e0, 204 + e1)
            tt(capD, Z17, o17("evD", c0, c1, 0), A.is_gt)
            tt(s("cap"), Z, s("ev"), A.is_gt)
            scan(o("sc1", 1 + e0, 1 + e1), o("dgv", e0, e1), capD, A.add, A.mult)
            tt(s("Mc"), Z, s("cap"), A.mult)
            tt(o("EQd", e0, e1), o("CB", e0, e1), o("sc1", e0, e1), A.is_equal)
            blocks = range(c0, min(c1, 11))
            for a in blocks:
                ts(o("EQ", 204 * a + 17 * a + 17, 204 * a + 204), o("CBh", 17 * a + 17, 204), 1424.0, A.add, o("sc1", 17 * a + 17, 17 * a + 18), A.is_equal)
            mm([(CN, o("Idb"), o("cK17", e0, e1))] * (bi == 0) + [(CN, o("N18"), capD), (CN, o("PB18"), o("EQd", e0, e1))] +
               [(o("CB", 204 + 17 * a + 17, 204 + e1), o("PB18"), o("EQ", 204 * a + 17 * a + 17, 204 * a + e1)) for a in blocks if a + 1 < c1], add=bi > 0)
            scan(o("sc2", e0, e1), CN, o("dgv", e0, e1), A.min, A.max)
            cp(lst("soff"), o("sc2", e0 + 16, e1, 17))
            act(o17("nw", c0, c1, 0), CN, F.Sign)
            if e1 < 204:
                mm([(o("CB", 204 + e1, 408), o("Idb"), o("cK17", e1, 204))] +
                   [(o("CB", 204 + e1, 408), o("PB18"), o("EQ", 204 * a + e1, 204 * a + 204)) for a in blocks], more=True)
            nw = o17("nw", c0, c1, 1)
            act(s("Wc"), s("Mc"), F.Exp, scale=LN32 / 4096)
            mm([(tb_(0), o("B16"), s("Wc"))])
            if CFG["G"][bi] == "S":
                act(s("Gm"), tb_(0), F.Sign, scale=-1.0, bias=o("thr"))
            else:
                ts(s("Gm"), tb_(0), o("thr"), A.is_lt, 2.0, A.mult)
            mm([(tb_(3), o("Idb"), s("cA")), (tb_(3), o("N18"), s("cap"))])
            tt(s("a1"), tb_(3), s("ev"), A.add)
            mm([(tb_(2), o("Idb"), s("cR")), (tb_(2), o("Idb"), o("NC", L * t + lo, L * t + hi)), (tb_(2), o("P18"), s("emp")),
                (tb_(2), o("P18"), s("cap")), (tb_(2), o("NB2k"), s("Gm"))])
            tt(s("a2"), tb_(2), s("H"), A.min)
            tt(ind("Ef", 0, nl + L, lst("soff")), s("a1"), s("a2"), A.max)
            due(t, "scat%d" % bi)
            act(s("z1"), Z, F.Copy)
            mm([(tb_(1), o("Idb"), s("z1")), (tb_(1), o("P16"), s("sig")), (tb_(1), o("N18"), s("emp")), (tb_(1), o("N18"), s("cap"))])
            act(s("Ws"), tb_(1), F.Exp, scale=SA, bias=o("bk"))
            mm([(tb_(4), o("BT"), s("Ws"))])
            tt(o17("sel", c0, c1, 1), tb_(4), s("Ws"), A.is_lt)
            tt(o17("pay", c0, c1, 1), o17("Z", 12 + c0, 12 + c1, 1), o17("sel", c0, c1, 1), A.mult)
            mm([(tb_(5), o("N18"), capD), (tb_(5), o("Bo"), o17("sel", c0, c1, 0)), (tb_(5), o("B16"), o17("pay", c0, c1, 0))])
            scan(o("sc3", e0, e1), o("RM", e0, e1), tb_(5), A.mult, A.max)
            tt(lst("a3"), o("sc3", e0 + 16, e1, 17), o("sc1", e0 + 17, e1 + 1, 17), A.add)
            ts(lst("winl"), o("sc2", e0 + 16, e1, 17), nl - 0.5, A.is_lt)
            tt(lst("tc"), lst("bmv"), lst("winl"), A.mult)
            tt(lst("vm"), lst("a3"), lst("tc"), A.add)
            if last:
                ts(lst("vfin"), lst("vm"), -float(PAD), A.add)
            else:
                cp(lst("voff"), lst("vm"))
                due(t, "voff%d" % bi)
                ts(lst("vmh"), lst("vm"), -1424.0, A.add)
            mm([(xb_(0), o("Idb"), yi(lo, hi)), (xb_(0), o("NB18"), nw)])
            act(s("Yw"), xb_(0), F.Relu, bias=15 * BIG)
            mm([(xb_(1), o("Idb"), s("x")), (xb_(1), o("NB18"), nw)])
            act(o("X", nl + lo, nl + hi), xb_(1), F.Relu, bias=15 * BIG)
            for c in range(3):
                if CFG["path"][c] == "S" and lo <= CH[c][0] < hi and not last:
                    turn(c, XB, 0 if bi == 0 else 192, True)
            mm([(xb_(2), o("Idb"), s("x")), (xb_(2), o("NegI"), s("Yw"))])
            act(s("x"), xb_(2), F.Abs)
            due(t, "x%d" % bi)
            mm([(xb_(3), o("Idb"), s("Mc")), (xb_(3), o("Idb"), s("Cf")), (xb_(3), o("NB18"), nw)])
            if not last:
                for c in range(3):
                    if CFG["path"][c] == "V" and lo <= CH[c][0] < hi:
                        repeat(*CH[c])
            if bi == 0:
                first_new = xb_(3)
            else:
                ts(o("Ef", nl, nl + lo), first_new, 1408.0 + 15 * BIG, A.add, 4095.0, A.max)
                due(t, "new")
                ts(o("Ef", nl + lo, nl + hi), xb_(3), 1408.0 + 15 * BIG, A.add, 4095.0, A.max)
                due(t, "new")
        if last:
            store("Y", T.ykids[:, 0:W - L], o("Ef", PAD, nl))
            store("S", T.ykids[:, W - L:W], o("Ef", nl, nl + L))
            store("Y", T.ynodes[:, :], o("X", PAD + M, PAD + W))
            store("S", T.ycand[:, :], o("x"))
            store("Y", T.yspot[:, :], o("vfin"))

    if "order" not in ORDER:
        ORDER["order"] = schedule(plan, dues)
    for i in ORDER["order"]:
        q, calls, reads, writes, kind, _d, _a = plan[i]
        if kind == "x":
            calls[0]()
        elif kind == "s":
            before("G", reads)
            calls[0]()
        else:
            emit_now(q, calls, reads, writes, dma=kind == "d")
    finish()
    g.wait_ge(T.sem.lsem, lcount[0])
